import numpy as np, ml_dtypes
CORES = [2,6,10,14,18,22,26,30]
N = 8
BF = ml_dtypes.bfloat16
def gentries(a):
    return np.ascontiguousarray(a.reshape(8, 16, -1).transpose(0, 2, 1)).reshape(8, -1)
def gtable(e):
    e = np.asarray(e); return np.ascontiguousarray(e.reshape(8, -1, 16).transpose(0, 2, 1)).reshape(128, -1).astype(np.int32)
V, S0, C, T = 3072, 256, 96, 3
A, B = (13, 12, 14), (11, 9, 10)
S = S0 + C * T
K = 64
def first(m):
    return np.take_along_axis(m, np.argmax(m < V, axis=-1)[..., None], -1)[..., 0]
def parts(rng):
    n, h = V // K, S0 // K
    vp = np.argsort(rng.random((8, V)), axis=1); w = np.full((N, 8, K, 16 * h), V); w[..., :n] = vp.reshape(8, K, n)
    m = np.take_along_axis(w, np.argsort(rng.random(w.shape), axis=-1), -1).reshape(N, 8, S0, 16)
    s = np.arange(S0)[:, None]; pos = s // h * n
    up = s + ((S0 - s) * rng.random(m.shape)).astype(np.int64); j = pos + ((V - pos) * rng.random(m.shape)).astype(np.int64)
    e1 = np.take_along_axis(first(m), up.reshape(N, 8, -1), 2).reshape(m.shape)
    e2 = np.take_along_axis(np.broadcast_to(vp, (N, 8, V)), j.reshape(N, 8, -1), 2).reshape(m.shape)
    z = rng.random(m.shape)
    return vp, m, np.where(z < 0.45, e1, np.where(z < 0.75, e2, np.where(z < 0.95, rng.integers(0, V, m.shape), V)))
def steps(rng, vp, dev, down):
    u = np.arange(K) + rng.integers(0, 24, (N, 8, 16, K)); cl = np.argsort(vp, axis=1) // (V // K)
    ix = np.take_along_axis(u, cl[None, :, None, :], 3) + 4
    i = np.arange(16)[:, None]; off = (i * (2 * rng.integers(0, 8, dev.shape) + 1) + rng.integers(0, 16, dev.shape)) % 16 < dev
    d = -1 if down else rng.integers(1, 4, ix.shape) * (2 * rng.integers(0, 2, ix.shape) - 1)
    return ix + np.where(off, d, 0)
def pack(rng, tab, ix, m, e):
    o = np.argsort(rng.random((N, 8, S0)), axis=2)[..., None]; e = np.where(np.any(m < V, axis=3, keepdims=True), e, V)
    m = np.take_along_axis(m, o, 2); e = np.take_along_axis(e, o, 2)
    return {"xs": np.take_along_axis(tab, ix, 3).astype(np.float32).reshape(N, 128, V).astype(BF),
            "mem0": np.stack([gtable(a.reshape(8, -1)) for a in m]), "inv0": np.stack([gtable(a.reshape(8, -1)) for a in e])}
def plain(rng):
    return np.sort(rng.standard_normal((N, 8, 16, 128)), axis=3) * np.exp2(rng.integers(-2, 3, (N, 8, 16, 1)))
def even(rng):
    return (np.arange(128) - 50) * np.exp2(rng.integers(-2, 3, (N, 8, 16, 1)))
def some(rng, share):
    return np.where(rng.random((N, 8, 1, V)) < share, rng.integers(1, 17, (N, 8, 1, V)), 0)
def chain(rng, vp, m, e, dev):
    n, h = V // K, S0 // K
    a = np.full((K, h, 16), V); a[:, :n // 16] = vp[7].reshape(K, n // 16, 16); a = a.reshape(S0, 16)
    s, row = np.argwhere(a == 0)[0]; a[s, row] = a[s, 1]; a[s, 1] = 0
    full = np.flatnonzero(a[:, 0] < V); sp = np.append(rng.permutation(full[full != s])[:C // 8 - 1], s)
    c = np.stack([np.append([0, 15], rng.permutation(np.arange(1, 15))) for b in sp]) ^ int(rng.integers(0, 16))
    m[:, 7] = a; dev[:, 7] = 0
    for q in range(N): dev[q, 7, 0, a[sp]] = 16 * ((c >> (q % 4)) & 1)
    z = rng.random((N, S0, 16))
    e[:, 7] = np.where(z < 0.5, a[:, :1], np.where(z < 0.75, rng.choice(a[sp, 0], z.shape), e[:, 7])); e[:, 7, :, 2] = a[:, 0]
def setup_inputs(rng):
    vp, m, e = parts(rng); share = rng.choice(np.array([0.004, 0.01, 0.02, 0.05]), (N, 8, 1, 1))
    return pack(rng, plain(rng), steps(rng, vp, some(rng, share), False), m, e)
def setup_inputs_room(rng):
    vp, m, e = parts(rng); dev = np.zeros((N, 8, 1, V), np.int64)
    for q in range(1, N, 2):
        for g in range(8):
            a = m[q - 1, g]; can = np.flatnonzero(np.sum(a < V, axis=1) > 1); row = np.argmax((a < V) * (rng.random(a.shape) + 0.5), axis=1)
            n = (C, C + 1, C - 1, S0, 1, 0, C, 2)[g] if q == 1 else int(rng.choice(np.array([0, 1, 2, C - 1, C, C + 1, S0])))
            s = rng.permutation(can)[:n]; dev[q, g, 0, a[s, row[s]]] = 16
    return pack(rng, even(rng), steps(rng, vp, dev, False), m, e)
def setup_inputs_ties(rng):
    vp, m, e = parts(rng); n, h = V // K, S0 // K
    j = np.arange(S0)[:, None] // h * n + rng.integers(0, n, m.shape)
    own = np.take_along_axis(np.broadcast_to(vp, (N, 8, V)), j.reshape(N, 8, -1), 2).reshape(m.shape)
    e = np.where(rng.random(m.shape) < 0.8, own, e); z = rng.random((N, 8, 1, V)); t = rng.integers(0, T, z.shape); one = rng.integers(0, 2, z.shape)
    dev = np.where(z < 0.02, 16 - np.array(B)[t] + one, np.where(z < 0.3, 16 - np.array(A)[t] + one, 0))
    chain(rng, vp, m, e, dev)
    return pack(rng, even(rng), steps(rng, vp, dev, True), m, e)
def setup_inputs_alike(rng):
    vp, m, e = parts(rng)
    m = np.where(rng.random(m.shape) < rng.random((N, 8, S0, 1)) * 1.2, m, V); m[:, :, 3::7, :15] = V; m[:, :, 5::11] = V
    lead = first(m); e[:, ::2] = rng.choice(np.array([0, V - 1, V // 2, V]), (N, 4, S0, 16))
    e[:, 1] = lead[:, 1, :, None]; e[:, 3] = lead[:, 3, S0 // 2, None, None]; e[:, 5] = V
    return pack(rng, plain(rng), steps(rng, vp, some(rng, 0.1), False), m, e)
def setup_inputs_crowd(rng):
    vp, m, e = parts(rng); share = rng.choice(np.array([0.1, 0.3, 0.8]), (N, 8, 1, 1)); share[rng.integers(0, N)] = 0.0; share[:, rng.integers(0, 8)] = 0.0
    return pack(rng, plain(rng), steps(rng, vp, some(rng, share), False), m, e)
def setup_inputs_spread(rng):
    vp, m, e = parts(rng); share = rng.choice(np.array([0.004, 0.01, 0.02, 0.05]), (N, 8, 1, 1)); w = (N, 8, 16, 128)
    z = rng.standard_normal(w); z = z * (np.abs(z) > 2.0 ** -8)
    size = np.exp2(rng.choice(np.array([-65, -62, -40, -20, -2, 0, 2, 20, 40, 80]), (N, 8, 16, 1)))
    tab = np.sort(z * np.exp2(rng.integers(-6, 7, w)) * (rng.random(w) > 0.0625), axis=3) * size
    return pack(rng, tab, steps(rng, vp, some(rng, share), False), m, e)
def check_inputs(d):
    bad = []
    x = np.abs(d["xs"].astype(np.float32))
    if not np.all((x == 0) | ((x >= 2.0 ** -100) & (x <= 2.0 ** 100))): bad.append("sizes of the numbers in xs")
    for k in ("mem0", "inv0"):
        if np.min(d[k]) < 0 or np.max(d[k]) > V: bad.append("range of " + k)
    z = np.sort(np.stack([gentries(a) for a in d["mem0"]]), axis=2)
    if np.any((z[..., 1:] == z[..., :-1]) & (z[..., 1:] < V)): bad.append("no variable twice in a group of mem0")
    a, b = d["mem0"].reshape(-1, 8, 16, S0), d["inv0"].reshape(-1, 8, 16, S0)
    if np.any(np.any(b < V, axis=2) & ~np.any(a < V, axis=2)): bad.append("no bounds in slots without members")
    return bad
def reference(xs, mem0, inv0):
    x = np.concatenate([xs.astype(np.float32).reshape(N, 8, 16, V), np.zeros((N, 8, 16, 1), np.float32)], axis=3)
    M = np.full((N, 8, S, 16), V, np.int64); I = np.full((N, 8, S, 16), V, np.int64)
    for r in range(N):
        M[r, :, :S0] = gentries(mem0[r]).reshape(8, S0, 16); I[r, :, :S0] = gentries(inv0[r]).reshape(8, S0, 16)
    for t in range(T):
        n = S0 + C * t
        for r in range(N):
            w = x[(r + t) % N]; m = M[r, :, :n].copy(); e = I[r, :, :n].copy(); lead = first(m)
            xl = np.take_along_axis(w, lead[:, None, :], 2)[..., None]
            xm = np.take_along_axis(w, m.reshape(8, 1, -1), 2).reshape(8, 16, n, 16); xe = np.take_along_axis(w, e.reshape(8, 1, -1), 2).reshape(8, 16, n, 16)
            e = np.where(np.sum(xl <= xe, axis=1) < A[t], V, e)
            leave = (m < V) & (np.sum(xm == xl, axis=1) < B[t])
            has = np.any(leave, axis=2).astype(np.int64); before = np.add.accumulate(has, axis=1) - has
            split = (has == 1) & (before < C); leave = leave & split[..., None]
            stay = np.where(leave, V, m); go = np.where(leave, m, V)
            M[r, :, :n] = stay; I[r, :, :n] = e
            for g in range(8):
                ids = np.flatnonzero(split[g]); k = len(ids)
                f = np.arange(V + 1); f[lead[g, ids]] = first(go[g, ids])
                M[r, g, n:n + k] = go[g, ids]; I[r, g, n:n + k] = np.where(e[g, ids] < V, f[e[g, ids]], stay[g, ids])
    return {"ym": np.stack([gtable(a.reshape(8, -1)) for a in M]).astype(np.float32), "yi": np.stack([gtable(a.reshape(8, -1)) for a in I]).astype(np.float32)}

@@ -1,0 +1,733 @@
+from concourse.bass import DstId, RemoteDMATransfer
+from concourse.mybir import AluOpType as ALU, ActivationFunctionType as ACT
+
+V, S0, C, NT, N = 3072, 256, 96, 3, 8
+AT, BT = (13, 12, 14), (11, 9, 10)
+S = S0 + C * NT
+HALF = 1536
+BIG = 4096.0
+FO = 3200
+
+NB = {"s0": 12, "s1": 12, "s2": 8, "d01": 12, "d02": 8, "d12": 8}
+FGS = 1
+DMAE = ("s0", "s1", "s2", "d02")
+NCH = 4
+LAGM, LAGE = 0, 0
+GCH = 32
+CY, CP, GA, SC = 1.04, 0.55, 1.56, 3.8
+LAT, LATS, HOP, ISSUE, XLAT = 110.0, 70.0, 2600.0, 700.0, 16000.0
+WIN, SLACK, MARGIN = 60.0, 400.0, 2500.0
+OFF = {"ms0": 6, "s0": 13, "s1": 3, "s2": 2, "md01": 6, "ms1": 5, "md12": 19, "p": 7, "r1": -2, "ed02": -2,
+       "ed01": -4, "es0": 9, "ms2": 5, "c": 5, "r2": -14, "ed12": 1}
+POOLS = {"cnt": [0, 1], "dif": [3, 4, 2], "xlp": [5], "log": [6, 7]}
+
+JOBS = {
+    "s0": (0, S0, "Qs", "Qs", 0, "xw"), "s1": (1, S0, "Qs1", "Qs1", 0, "xw"), "s2": (2, S0, "Qs", "Qs", 0, "xw2"),
+    "d01": (1, C, "Qm01", "Qe01", S0, "xw"), "d02": (2, C, "Qm0", "Qe0", S0, "xw2"),
+    "d12": (2, C, "Qm1", "Qe1", S0 + C, "xw2")}
+
+BUF = {}
+
+
+def _decl(names, cols, dtype):
+    for nm in names.split():
+        BUF[nm] = (cols, dtype)
+
+
+_decl("xw xw2", V + 16, "bfloat16")
+_decl("mi", 2 * S0, "int32")
+_decl("U E LR YM YI", S, "float32")
+_decl("F", 2 * FO, "float32")
+_decl("Qs Qs1", 2 * S0 + 16, "uint16")
+_decl("Qm0 Qm1 Qm01", 136, "uint16")
+_decl("Qe0 Qe1 Qe01 EG", C, "uint16")
+for _t in range(NT):
+    _decl("TW%d" % _t, S0 + C * _t + C, "bfloat16")
+    _decl("TD%d" % _t, S0 + C * _t, "bfloat16")
+for _j, _v in JOBS.items():
+    _decl("xl_%s" % _j, _v[1], "bfloat16")
+    _decl("cm_%s ce_%s xe_%s" % (_j, _j, _j), 16 * _v[1], "bfloat16")
+    if _v[0] == 1:
+        _decl("am_%s ae_%s" % (_j, _j), _v[1], "bfloat16")
+_decl("G2 Z2", 2 * S0, "float32")
+_decl("W DG SG cap rm R R16", S0, "float32")
+_decl("gcb", S0 + 2 * C, "bfloat16")
+_decl("AS AB", S0, "bfloat16")
+_decl("hb", 32, "bfloat16")
+_decl("junk", 192, "bfloat16")
+_decl("bc cumT zero", 32, "float32")
+_decl("fine C96", C, "bfloat16")
+_decl("acc tq tt s1 Kc Kb", 8, "float32")
+_decl("ids ll", 8 * NT, "uint16")
+_decl("al permd", 8, "uint16")
+_decl("ug lg ls sm eg", C, "float32")
+_decl("GO stay LG sl", C * NT, "float32")
+_decl("FG", 16 * C, "float16")
+_decl("I NI BO SU", 128, "bfloat16")
+_decl("BO32 MT M4", 128, "float32")
+_decl("B", 144, "bfloat16")
+_decl("Bh", 144, "float16")
+_decl("PI", 8, "int32")
+_decl("PF CB low", 16, "float32")
+_decl("dup", 32, "uint16")
+_decl("perm", 16, "uint16")
+
+SCRATCH = {"b_" + nm: ("sbuf", [128, c], d) for nm, (c, d) in BUF.items()}
+for _b in range(8):
+    SCRATCH["P%d" % _b] = ("psum", [128, 512], "float32")
+
+OPS = []
+TAG = [""]
+SEMS = ["sv", "ss", "sp", "sg", "sent", "xa"]
+
+
+def A(name, a=0, b=None, s=1):
+    return ("ap", name, a, BUF[name][0] if b is None else b, s)
+
+
+def IND(win, off):
+    return ("ind", win, off)
+
+
+def _isap(x):
+    return isinstance(x, tuple) and x[0] in ("ap", "ind")
+
+
+def _n(x):
+    return 16 * _n(x[2]) if x[0] == "ind" else (x[3] - x[2] + x[4] - 1) // x[4]
+
+
+def _ps(x):
+    return _isap(x) and x[0] == "ap" and x[1][0] == "@"
+
+
+def _two(x):
+    return x[0] == "ap" and not _ps(x) and BUF[x[1]][1] in ("bfloat16", "float16", "uint16")
+
+
+def _regs(x):
+    return _regs(x[1]) + _regs(x[2]) if x[0] == "ind" else [(x[1], x[2], x[3])]
+
+
+def op(eng, fn, outs, ins, args, cost, kw=None, lat=0.0, sem=None, dst=None):
+    wr, rd = [], []
+    for o in outs:
+        if o[0] == "ind":
+            wr += _regs(o[1])
+            rd += _regs(o[2])
+        else:
+            wr += _regs(o)
+    for i in ins:
+        if _isap(i):
+            rd += _regs(i)
+    OPS.append({"eng": eng, "fn": fn, "args": args, "kw": kw or {}, "wr": wr, "rd": rd, "cost": cost, "lat": lat,
+                "sem": sem, "dst": dst, "tag": TAG[0]})
+
+
+def _vcost(out, in0, per):
+    if out[0] == "ind":
+        return 60 + SC * _n(out) * CY
+    if in0[0] == "ind":
+        return 60 + GA * _n(out) * CY
+    return 40 + max(64, per * _n(in0)) * CY
+
+
+def tt(out, a, b, o):
+    op("v", "tensor_tensor", [out], [a, b], [out, a, b, o], _vcost(out, a, 1 if _ps(a) or _ps(b) else 2))
+
+
+def ts(out, a, s1, s2, o0, o1=None):
+    args = [out, a, s1, s2, o0] + ([] if o1 is None else [o1])
+    op("v", "tensor_scalar", [out], [a, s1, s2], args, _vcost(out, a, 0.5 if _two(out) and _two(a) else 1))
+
+
+def cp(out, a):
+    op("v", "tensor_copy", [out], [a], [out, a], _vcost(out, a, 0.5 if _two(out) and _two(a) else 1))
+
+
+def ms(out, c):
+    op("v", "memset", [out], [], [out, c], _vcost(out, out, 0.5 if _two(out) else 1))
+
+
+def scan(out, d0, d1, init, o0, o1):
+    op("v", "tensor_tensor_scan", [out], [d0, d1], [out, d0, d1, init, o0, o1], _vcost(out, d0, 1))
+
+
+def vtranspose(n):
+    op("v", "transpose", [A("Z2", 0, n)], [A("G2", 0, n)], [A("Z2", 0, n), A("G2", 0, n)], 40 + n * CY)
+
+
+def act(out, a, f, bias=0.0, scale=1.0, accum=None):
+    kw = {} if f == ACT.Copy else {"bias": bias, "scale": scale}
+    outs = [out]
+    if accum is not None:
+        kw["accum_out"] = accum
+        outs.append(accum)
+    cost = 80 + GA * _n(out) * CY if a[0] == "ind" else 80 + max(64, _n(out)) * CY
+    op("s", "activation", outs, [a, bias, scale], [out, a, f], cost, kw)
+
+
+def mm(out, l, r, start, stop):
+    four = 4 if BUF[r[1]][1] == "float32" else 1
+    op("p", "matmul", [out], [l, r], [out, l, r, start, stop], 10 + four * max(64, _n(r)) * CP)
+
+
+def iota(out, pat, base, cm):
+    kw = {} if BUF[out[1]][1] == "int32" else {"allow_small_or_imprecise_dtypes": True}
+    op("g", "iota", [out], [], [out, pat, base, cm], 160 + 2 * _n(out) * CY, kw)
+
+
+def aff(out, a, pat, cmp_op, fill, base, cm):
+    op("g", "affine_select", [out], [a], [out, a, pat, cmp_op, fill, base, cm], 210 + 2 * _n(out) * CY)
+
+
+def dma(eng, out, a, nbytes, add=False):
+    sem = "d%d" % len(SEMS)
+    SEMS.append(sem)
+    outs = [out] if out[1] in BUF else []
+    ins = [a] if a[1] in BUF else []
+    if add:
+        op(eng, "dma_start", outs, ins + outs, [out, a], ISSUE, {"accum_op": ALU.add}, 2200 + nbytes / 95.0, sem)
+    else:
+        op(eng, "dma_start", outs, ins, [out, a], 80.0, lat=2000 + nbytes / 190.0, sem=sem)
+
+
+def send(dst, out, a, a2=None):
+    sem = "r%d" % len(SEMS)
+    SEMS.append(sem)
+    op("g", "remote_dma", [out], [a, a2], [out, a] + ([] if a2 is None else [a2]), ISSUE,
+       lat=HOP + 256 * _n(a) / 60.0, sem=sem, dst=dst)
+
+
+def col(name, c):
+    return A(name, c, c + 1)
+
+
+def sel(name, i):
+    return A(name, 15 - i, 143 - i)
+
+
+BIASCOL = {}
+
+
+def constants():
+    iota(col("PI", 0), [[0, 1]], 0, 1)
+    ms(A("M4"), -BIG)
+    aff(A("M4"), A("M4"), [[-16, 8], [0, 16]], ALU.is_ge, 0.0, 0, 1)
+    aff(A("M4"), A("M4"), [[16, 8], [0, 16]], ALU.is_ge, 0.0, 15, -1)
+    aff(A("MT"), A("M4"), [[1, 128]], ALU.is_gt, 0.0, 0, -1)
+    aff(A("MT"), A("MT"), [[1, 128]], ALU.not_equal, 1.0, 0, -1)
+    iota(A("R"), [[1, S0]], 0, 0)
+    iota(A("R16"), [[0, 16], [1, 16]], 0, 0)
+    for c, m in ((1, 15), (2, 112), (3, 16), (4, 7)):
+        ts(col("PI", c), col("PI", 0), m, None, ALU.bitwise_and)
+    ts(col("PI", 5), col("PI", 0), 3, 1, ALU.logical_shift_right, ALU.bitwise_and)
+    cp(A("PF", 0, 6), A("PI", 0, 6))
+    pb, pg, pc = col("PF", 1), col("PF", 2), col("PF", 3)
+    ts(col("PF", 6), pb, 32.0, pc, ALU.mult, ALU.add)
+    ts(col("PF", 7), col("PF", 4), 5.0, 32.0, ALU.min, ALU.mult)
+    ts(col("PF", 8), col("PF", 7), pc, col("PF", 5), ALU.add, ALU.add)
+    ts(A("dup", 0, 32, 2), A("R", 0, S0, 16), pb, None, ALU.add)
+    ts(A("dup", 1, 32, 2), A("R", 0, S0, 16), pb, None, ALU.add)
+    ts(A("perm"), A("R", 0, 16), col("PF", 6), None, ALU.add)
+    ts(A("permd"), A("R", 0, 16, 2), col("PF", 8), None, ALU.add)
+    act(A("BO32"), A("M4"), ACT.Identity, 0.0, -1.0 / BIG)
+    act(A("BO"), A("M4"), ACT.Identity, 0.0, -1.0 / BIG)
+    aff(A("SU"), A("BO"), [[-1, 128]], ALU.is_gt, 0.0, 0, 1)
+    ms(A("zero"), 0.0)
+    ms(A("cumT"), 65536.0)
+    ts(A("B"), A("R", 0, 144), pg, 15.0, ALU.subtract, ALU.is_equal)
+    ts(A("Bh"), A("B"), 1.0 / 16, None, ALU.mult)
+    ts(A("I"), A("R", 0, 128), col("PF", 0), None, ALU.is_equal)
+    act(A("NI"), A("I"), ACT.Identity, 0.0, -1.0)
+    ts(A("cap"), A("R16"), pb, None, ALU.is_equal)
+    act(A("W"), A("R"), ACT.Identity, float(V + 1))
+    tt(A("cap"), A("cap"), A("W"), ALU.mult)
+    act(A("rm"), A("R16"), ACT.Sign)
+    act(A("Kc", 0, 6), A("R", 0, C, 16), ACT.Identity, pb)
+    act(A("Kb", 0, 6), A("Kc", 0, 6), ACT.Identity, 0.5)
+    ms(A("C96"), HALF / 16.0)
+    ms(col("CB", 0), 2.0 ** -112)
+    for j, v in JOBS.items():
+        key = (NB[j], AT[v[0]])
+        if key not in BIASCOL:
+            c = 1 + len(BIASCOL)
+            BIASCOL[key] = c
+            ts(col("CB", c), pb, float(key[0]), 2 * BIG * (key[1] - 16), ALU.is_lt, ALU.mult)
+            act(col("CB", c), col("CB", c), ACT.Identity, 2 * BIG * key[1])
+    act(col("CB", 14), col("CB", BIASCOL[(NB["s1"], AT[1])]), ACT.Identity, 0.0, 0.5 / BIG)
+    ms(A("low"), -2.0 ** 99)
+    act(A("xw", V), A("low"), ACT.Identity, 0.0, 4.0)
+    act(A("xw2", V), A("low"), ACT.Identity, 0.0, 4.0)
+    ms(A("U", S0), 0.0)
+    ms(A("E", S0), 2 * BIG)
+    ms(A("LR", S0), 65536.0)
+    for t in range(NT):
+        ms(A("TW%d" % t, S0 + C * t), 0.0)
+    ms(A("Qm0", 128), 0)
+    for a in range(0, 2 * FO, 400):
+        iota(A("F", a, a + 400), [[1, 400]], a % FO - HALF, 0)
+
+
+def leaders(src, n, tag, lr, lst):
+    pa, pb = A("@log" + tag + "a", 0, n), A("@log" + tag + "b", 0, n)
+    mm(pa, A("MT"), src, True, True)
+    act(A("W", 0, n), pa, ACT.Relu)
+    mm(pb, A("BO32"), A("W", 0, n), True, True)
+    if lst is not None:
+        tt(A("DG", 0, n), pb, A("cap", 0, n), ALU.min)
+    act(lr, pb, ACT.Identity, float(V), -1.0)
+    if lst is not None:
+        scan(A("SG", 0, n), A("rm", 0, n), A("DG", 0, n), 0.0, ALU.mult, ALU.add)
+        ts(lst, A("SG", 15, n, 16), -1.0, float(V), ALU.mult, ALU.add)
+
+
+def prepare():
+    dma("y", A("mi", 0, S0), ("ap", "mem0", 0, S0, 1), 131072)
+    dma("s", A("mi", S0), ("ap", "inv0", 0, S0, 1), 131072)
+    dma("y", A("xw", 0, V), ("ap", "xs", 0, V, 1), 786432)
+    OPS[-1]["after"] = len(OPS) - 3
+    ts(A("U", 0, S0), A("mi", 0, S0), -1.0, float(V), ALU.mult, ALU.add)
+    act(A("G2"), IND(A("U", 0, S0), A("dup")), ACT.Identity, float(V), -1.0)
+    cp(A("Qs", S0 + 16), A("mi", S0))
+    cp(A("E", 0, S0), A("mi", S0))
+    leaders(A("U", 0, S0), S0, "p", A("LR", 0, S0), A("Qs", S0, S0 + 16))
+    vtranspose(2 * S0)
+    cp(A("Qs", 0, S0), IND(A("Z2"), A("perm")))
+    send(1, A("Qs1"), A("Qs"))
+    op("g", "relay", [A("xw2", 0, V)], [A("xw", 0, V)], [], NCH * ISSUE, lat=XLAT, sem="xa", dst=-2)
+
+
+def members(j):
+    t, n, q, _, s0, xw = JOBS[j]
+    w = 16 if n == S0 else 8
+    k = n // 16
+    xl = A("xl_" + j)
+    cnt = A("@cntm" + j, 0, n)
+    act(xl, IND(A(xw), A(q, 16 * w, 16 * w + k)), ACT.Copy)
+    first = len(OPS)
+    for i in range(16):
+        tt(A("cm_" + j, i * n, (i + 1) * n), IND(A(xw), A(q, i * w, i * w + k)), xl, ALU.is_equal)
+    for i in range(16):
+        mm(cnt, sel("B", i), A("cm_" + j, i * n, (i + 1) * n), i == 0, i == 15)
+        OPS[-1]["after"] = first + min(15, i + LAGM)
+    home = A("TW%d" % t, s0, s0 + n)
+    if j == "s1":
+        ts(A("am_" + j), cnt, float(BT[t]), 2 * BIG, ALU.is_lt, ALU.mult)
+        return
+    act(A("am_" + j) if t == 1 else home, cnt, ACT.Relu, BIG * BT[t], -BIG)
+    if t == 1:
+        send(-1, home, A("am_" + j))
+
+
+def bounds(j):
+    t, n, _, q, s0, xw = JOBS[j]
+    o = S0 + 16 if n == S0 else 0
+    xl = A("xl_" + j)
+    cnt = A("@cnte" + j, 0, n)
+    ch = GCH if n == S0 else C // 2
+    for a in range(0, n, ch):
+        act(A("xe_" + j, 16 * a, 16 * (a + ch)), IND(A(xw), A(q, o + a, o + a + ch)), ACT.Copy)
+    nb = NB[j]
+    per_bank = 2 if n == S0 else 4
+    units = [("b", list(range(i, min(nb, i + per_bank)))) for i in range(0, nb, per_bank)]
+    cs = list(range(nb, 16))
+    seq = []
+    while units or cs:
+        if units:
+            seq.append(units.pop(0))
+        if cs:
+            seq.append(("c", [cs.pop(0)]))
+    if nb < 16:
+        mm(A("@xlp" + j, 0, n), A("I"), xl, True, True)
+    made = []
+    for kind, rows in seq:
+        if kind == "b":
+            bank = "@dif%s_%d" % (j, rows[0])
+            for z, i in enumerate(rows):
+                mm(A(bank, z * n, (z + 1) * n), A("I"), A("xe_" + j, i, 16 * n, 16), True, False)
+                mm(A(bank, z * n, (z + 1) * n), A("NI"), xl, False, True)
+            act(A("ce_" + j, rows[0] * n, (rows[-1] + 1) * n), A(bank, 0, len(rows) * n), ACT.Sign, col("CB", 0))
+        else:
+            i = rows[0]
+            tt(A("ce_" + j, i * n, (i + 1) * n), A("xe_" + j, i, 16 * n, 16), A("@xlp" + j, 0, n), ALU.is_ge)
+        made += [(i, len(OPS) - 1) for i in rows]
+    for z, (i, _) in enumerate(made):
+        mm(cnt, sel("B", i), A("ce_" + j, i * n, (i + 1) * n), z == 0, z == 15)
+        OPS[-1]["after"] = made[min(15, z + LAGE)][1]
+    home = A("TD%d" % t, s0, s0 + n)
+    if j == "s1":
+        ts(A("ae_" + j), cnt, col("CB", 14), -BIG, ALU.is_ge, ALU.mult)
+        send(-1, A("AS"), A("am_" + j), A("ae_" + j))
+        return
+    act(A("ae_" + j) if t == 1 else home, cnt, ACT.Relu, col("CB", BIASCOL[(nb, AT[t])]), -2 * BIG)
+    if t == 1:
+        send(-1, home, A("ae_" + j))
+
+
+def parts(t):
+    return [(0, S0)] + [(S0 + C * z, S0 + C * (z + 1)) for z in range(t)]
+
+
+def per(name, t):
+    w = BUF[name][0] // NT
+    return A(name, w * t, w * t + (6 if w == 8 else w))
+
+
+def positions(t):
+    n = S0 + C * t
+    na = n // 16
+    h, u, f = A("@logh%d" % t, 0, na), "@logu%d" % t, A("@logi%d" % t, 0, 6)
+    for b in range(16):
+        mm(h, sel("B", b), A("gcb", b, n, 16), b == 0, b == 15)
+    act(A("hb", 0, na), h, ACT.Sign)
+    mm(A(u, 0, na), A("BO"), A("hb", 0, na), True, True)
+    mm(A(u, 32, 32 + na), A("SU"), A("hb", 0, na), True, True)
+    bc = A("bc", 0, na)
+    scan(bc, A(u, 0, na), A("zero", 0, na), 0.0, ALU.add, ALU.add)
+    tt(A("cumT", 0, na), bc, A(u, 32, 32 + na), ALU.subtract)
+    for a in range(6):
+        act(A("junk", 32 * a, 32 * a + na), bc, ACT.Sign, col("Kb", a), -1.0, col("acc", a))
+    ts(A("al", 0, 6), A("acc", 0, 6), 0.5, na / 2.0, ALU.mult, ALU.add)
+    tt(A("fine"), IND(A("cumT"), A("al", 0, 6)), A("R", 0, C), ALU.is_le)
+    ts(A("tq", 0, 6), A("Kc", 0, 6), col("bc", na - 1), 0.0, ALU.subtract, ALU.max)
+    act(A("tt", 0, 6), A("acc", 0, 6), ACT.Identity, 8.0 * na, 8.0)
+    tt(A("tq", 0, 6), A("tq", 0, 6), A("tt", 0, 6), ALU.add)
+    for b in range(16):
+        mm(f, sel("B", b), A("fine", b, C, 16), b == 0, b == 15)
+    tt(A("s1", 0, 6), f, A("tq", 0, 6), ALU.add)
+    cp(per("ids", t), A("s1", 0, 6))
+
+
+def split(t):
+    n = S0 + C * t
+    tw = "TW%d" % t
+    last = t == NT - 1
+    ids, go, stay, sl, lg, ll = (per(x, t) for x in ("ids", "GO", "stay", "sl", "LG", "ll"))
+    if t == 1:
+        ts(A(tw, 0, S0), A("AS"), 0.0, None, ALU.max)
+    for a, b in parts(t):
+        tt(A("gcb", a, b), A(tw, a, b), A("U", a, b), ALU.min)
+    if last:
+        act(A("YM", 0, n), A("U", 0, n), ACT.Identity, float(V), -1.0)
+    positions(t)
+    cp(A("ug"), IND(A("U", 0, n + C), ids))
+    tt(go, IND(A(tw), ids), A("ug"), ALU.min)
+    if not last:
+        act(A("G2", 0, 2 * C), IND(go, A("dup", 0, 12)), ACT.Identity, float(V), -1.0)
+    leaders(go, C, "n%d" % t, sl, None if last else A("Qm%d" % t, 128, 134))
+    if not last:
+        vtranspose(2 * C)
+        cp(A("Qm%d" % t, 0, 128), IND(A("Z2", 0, 2 * C), A("permd")))
+    if t == 0:
+        send(1, A("Qm01"), A("Qm0"))
+    tt(stay, A("ug"), go, ALU.subtract)
+    if last:
+        ts(IND(A("YM"), ids), stay, -1.0, float(V), ALU.mult, ALU.add)
+        act(A("YM", n, n + C), go, ACT.Identity, float(V), -1.0)
+        dma("y", ("ap", "ym", 0, S, 1), A("YM"), 278528)
+    else:
+        cp(IND(A("U", 0, n + C), ids), stay)
+        act(A("U", n, n + C), go, ACT.Copy)
+    tt(A("lg"), IND(A("LR", 0, n + C), ids), A("cap", 0, C), ALU.min)
+    if not last:
+        act(lg, IND(A("LR", 0, n + C), ids), ACT.Copy)
+        act(A("LR", n, n + C), sl, ACT.Copy)
+    scan(A("ls"), A("rm", 0, C), A("lg"), 0.0, ALU.mult, ALU.add)
+    cp(ll, A("ls", 15, C, 16))
+
+
+def rename(t):
+    n = S0 + C * t
+    last = t == NT - 1
+    ids, stay, sl, lg, ll = (per(x, t) for x in ("ids", "stay", "sl", "LG", "ll"))
+    ts(IND(A("F", 0, FO), ll), sl, 1.0, float(-HALF), ALU.mult, ALU.add)
+    for a, b in parts(t):
+        if t == 1 and a == 0:
+            act(A("AB"), A("AS"), ACT.Abs)
+            act(A("TD1", 0, S0), A("AB"), ACT.Abs, -2 * BIG, 2.0)
+        if any(v[0] == t and v[4] == a for j, v in JOBS.items() if j in DMAE):
+            dma("g", A("E", a, b), A("TD%d" % t, a, b), 512 * (b - a), True)
+        else:
+            tt(A("E", a, b), A("TD%d" % t, a, b), A("E", a, b), ALU.max)
+    act(A("sm"), stay, ACT.Identity, float(V + FO), -1.0)
+    tt(A("eg"), IND(A("E", 0, n + C), ids), A("sm"), ALU.min)
+    cp(A("EG"), A("eg"))
+    if last:
+        ts(A("YI", 0, n), A("E", 0, n), float(V), None, ALU.min)
+        dma("y", ("ap", "yi", 0, n, 1), A("YI", 0, n), 229376)
+    h = C // 2
+    for a in (0, h):
+        if a < FGS * h:
+            act(A("FG", 16 * a, 16 * (a + h)), IND(A("F"), A("EG", a, a + h)), ACT.Copy)
+        else:
+            cp(A("FG", 16 * a, 16 * (a + h)), IND(A("F"), A("EG", a, a + h)))
+    bank = A("@logf%d" % t, 0, C)
+    for i in range(16):
+        mm(bank, sel("Bh", i), A("FG", i, 16 * C, 16), i == 0, False)
+    mm(bank, A("BO"), A("C96"), False, True)
+    if last:
+        act(A("YI", n, n + C), bank, ACT.Copy)
+        dma("y", ("ap", "yi", n, S, 1), A("YI", n, S), 49152)
+    else:
+        cp(A("Qe%d" % t), bank)
+        act(A("E", n, n + C), bank, ACT.Copy)
+        if t == 0:
+            send(1, A("Qe01"), A("Qe0"))
+        ts(IND(A("F", 0, FO), ll), lg, 1.0, float(-HALF), ALU.mult, ALU.add)
+
+
+def program():
+    steps = [("c", constants, None), ("p", prepare, None)]
+    for j in ("s0", "s1", "s2", 0, "d01", "d02", 1, "d12", 2):
+        steps += [("m", members, j), ("e", bounds, j)] if j in JOBS else [("s", split, j), ("r", rename, j)]
+    for tag, f, x in steps:
+        TAG[0] = tag + ("" if x is None else str(x))
+        if x is None:
+            f()
+        else:
+            f(x)
+
+
+def dependencies():
+    hist = {}
+    for k, o in enumerate(OPS):
+        deps = {}
+        acc = [(r, True) for r in o["wr"]] + [(r, False) for r in o["rd"]]
+        for (nm, a, b), w in acc:
+            for (j, a2, b2, w2) in hist.get(nm, []):
+                same = OPS[j]["eng"] == o["eng"] and OPS[j]["sem"] is None
+                if nm[0] == "@" or (a < b2 and a2 < b and (w or w2)):
+                    deps[j] = deps.get(j, False) or not same or ((w or w2) and o["eng"] != "p")
+        for (nm, a, b), w in acc:
+            hist.setdefault(nm, []).append((k, a, b, w))
+        if "after" in o:
+            deps.setdefault(o["after"], False)
+        o["deps"] = deps
+        o["banks"] = sorted(set(r[0] for r, w in acc if r[0][0] == "@"))
+    return {nm: [h[0] for h in v] for nm, v in hist.items() if nm[0] == "@"}
+
+
+def schedule():
+    users = dependencies()
+    n = len(OPS)
+    succ = [[] for _ in range(n)]
+    for k, o in enumerate(OPS):
+        for j in o["deps"]:
+            succ[j].append(k)
+    prio = [0.0] * n
+    behind = {}
+    for k in range(n - 1, -1, -1):
+        o = OPS[k]
+        prio[k] = o["cost"] + o["lat"] + max([prio[s] + LAT for s in succ[k]] + [0.0])
+        key = (o["eng"], o["wr"][0][0]) if o["wr"] and o["wr"][0][0][:3] in ("cm_", "ce_", "xe_") else None
+        if key in behind:
+            prio[k] = max(prio[k], o["cost"] + behind[key])
+        if key:
+            behind[key] = prio[k]
+    for k in range(n):
+        prio[k] += 1000.0 * OFF.get(OPS[k]["tag"], 0)
+    left = [len(o["deps"]) for o in OPS]
+    ready = [k for k in range(n) if left[k] == 0]
+    free = {e: 0.0 for e in "vspgy"}
+    end = [0.0] * n
+    holder = {b: None for b in range(8)}
+    bound = {}
+    todo = {nm: len(set(v)) for nm, v in users.items()}
+    order = []
+
+    def avail(j, eng, hard):
+        if not hard:
+            return 0.0
+        return end[j] + OPS[j]["lat"] + (LATS if OPS[j]["eng"] == eng else LAT)
+
+    while ready:
+        cand = []
+        for k in ready:
+            o = OPS[k]
+            t = max([avail(j, o["eng"], h) for j, h in o["deps"].items()] + [0.0])
+            pick = None
+            ok = True
+            for nm in o["banks"]:
+                if nm not in bound:
+                    opts = [(0.0 if holder[b] is None else avail(users[holder[b]][-1], o["eng"], True), b)
+                            for b in POOLS[nm[1:4]] if holder[b] is None or todo[holder[b]] == 0]
+                    if opts:
+                        pick = (nm, min(opts)[1])
+                        t = max(t, min(opts)[0])
+                    else:
+                        ok = False
+            if ok:
+                cand.append((max(t, free[o["eng"]]), k, pick))
+        est = {c[1]: c[0] for c in cand}
+        soon = {e: [] for e in free}
+        horizon = min(cand)[0] + 2000.0
+        seen = {}
+        front = [c[1] for c in cand]
+        while front:
+            j = front.pop()
+            if est[j] > horizon:
+                continue
+            soon[OPS[j]["eng"]].append(j)
+            for k in succ[j]:
+                seen[k] = seen.get(k, 0) + 1
+                if seen[k] == left[k]:
+                    o = OPS[k]
+                    t = free[o["eng"]]
+                    for i, h in o["deps"].items():
+                        t = max(t, est[i] + OPS[i]["cost"] + (OPS[i]["lat"] + LAT if h else 0) if i in est
+                                else avail(i, o["eng"], h))
+                    est[k] = t
+                    front.append(k)
+        clear = [c for c in cand if not any(
+            prio[h] > prio[c[1]] + MARGIN and est[h] < c[0] + OPS[c[1]]["cost"] - SLACK for h in soon[OPS[c[1]]["eng"]])]
+        cand = clear or cand
+        t0, k0, _ = min(cand)
+        eng = OPS[k0]["eng"]
+        near = [c for c in cand if OPS[c[1]]["eng"] == eng and c[0] <= t0 + WIN]
+        t, k, pick = max(near, key=lambda c: prio[c[1]])
+        o = OPS[k]
+        if pick is not None:
+            nm, b = pick
+            if holder[b] is not None:
+                o["deps"][users[holder[b]][-1]] = True
+            holder[b] = nm
+            bound[nm] = b
+        for nm in o["banks"]:
+            todo[nm] -= 1
+        o["t"] = t
+        end[k] = t + o["cost"]
+        free[eng] = end[k]
+        order.append(k)
+        ready.remove(k)
+        for s in succ[k]:
+            left[s] -= 1
+            if left[s] == 0:
+                ready.append(s)
+    return order, bound, max(end[k] + OPS[k]["lat"] for k in range(n))
+
+
+def waits(order):
+    know = {e: {} for e in "vspgy"}
+    pos = {e: 0 for e in "vspgy"}
+    for k in order:
+        o = OPS[k]
+        kn = know[o["eng"]]
+        need = []
+        for j in sorted((j for j, h in o["deps"].items() if h), key=lambda j: -OPS[j]["t"]):
+            d = OPS[j]
+            key = d["sem"] or d["eng"]
+            if kn.get(key, -1) >= d["pos"]:
+                continue
+            need.append(j)
+            kn[key] = d["pos"]
+            d["mark"] = True
+            if d["dst"] is None:
+                for a, b in d["clock"].items():
+                    if kn.get(a, -1) < b:
+                        kn[a] = b
+        o["need"] = need
+        o["pos"] = pos[o["eng"]]
+        pos[o["eng"]] += 1
+        o["clock"] = dict(kn)
+    count = {e: 0 for e in "vspg"}
+    for k in order:
+        o = OPS[k]
+        if o["sem"] is None and o.get("mark"):
+            count[o["eng"]] += 1
+            o["count"] = count[o["eng"]]
+
+
+program()
+ORDER, BANK, SPAN = schedule()
+waits(ORDER)
+SEMAPHORES = SEMS + ["h%d" % c for c in range(NCH)]
+
+
+def rank_program(g, core, T, topo):
+    rank = T.rank_of(core)
+
+    def lanes(src, dst):
+        return topo.engines(src, dst)[:8]
+
+    def bits(es):
+        return sum(1 << e for e in es)
+
+    def helper(r):
+        src, dst = T.cores[r], T.cores[(r - 2) % N]
+        return [c for c in topo.cores_of(src) if T.rank_of(c) is None and topo.die(c) == topo.die(src)
+                and topo.may_write(c, dst)][0]
+
+    piece = V // NCH
+    if rank is None:
+        for r in range(N):
+            if helper(r) == core:
+                dst = T.cores[(r - 2) % N]
+                rid, pid, _ = topo.addr(dst)
+                es = lanes(core, dst)
+                for c in range(NCH):
+                    g.wait_ge(T.sem["h%d" % c], len(topo.engines(T.cores[r], core)[-8:]))
+                    x = T.b_xw2[:, c * piece:(c + 1) * piece]
+                    g.remote_dma(x, x, T.sem.xa, T.sem.sent, pid, rid, bits(es))
+                g.wait_ge(T.sem.sent, NCH * len(es))
+        return
+    queue = {"v": g.vector, "s": g.scalar, "p": g.tensor, "g": g, "y": g.sync}
+
+    def view(x):
+        if not _isap(x):
+            return x
+        if x[0] == "ind":
+            return view(x[1]).indirect(view(x[2]))
+        buf = T["P%d" % BANK[x[1]]] if x[1][0] == "@" else T[("b_" if x[1] in BUF else "") + x[1]]
+        return buf[:, x[2]:x[3]:x[4]] if x[4] != 1 else buf[:, x[2]:x[3]]
+
+    calls = {
+        "tensor_tensor": g.vector.tensor_tensor, "tensor_scalar": g.vector.tensor_scalar,
+        "tensor_copy": g.vector.tensor_copy, "memset": g.vector.memset,
+        "tensor_tensor_scan": g.vector.tensor_tensor_scan, "transpose": g.vector.transpose,
+        "activation": g.scalar.activation, "matmul": g.tensor.matmul,
+        "iota": g.iota, "affine_select": g.affine_select}
+    sent = 0
+    for k in ORDER:
+        o = OPS[k]
+        q = queue[o["eng"]]
+        for j in o["need"]:
+            d = OPS[j]
+            if d["fn"] == "relay":
+                q.wait_ge(T.sem.xa, NCH * len(lanes(helper((rank + 2) % N), core)))
+            elif d["dst"] is not None:
+                q.wait_ge(T.sem[d["sem"]], len(lanes(T.cores[(rank - d["dst"]) % N], core)))
+            elif d["sem"] is not None:
+                q.wait_ge(T.sem[d["sem"]], 16)
+            else:
+                q.wait_ge(T.sem["s" + d["eng"]], d["count"])
+        args = [view(a) for a in o["args"]]
+        if o["fn"] == "relay":
+            hp = helper(rank)
+            rid, pid, _ = topo.addr(hp)
+            es = topo.engines(core, hp)[-8:]
+            for c in range(NCH):
+                g.remote_dma(T.b_xw2[:, c * piece:(c + 1) * piece], T.b_xw[:, c * piece:(c + 1) * piece],
+                             T.sem["h%d" % c], T.sem.sent, pid, rid, bits(es))
+                sent += len(es)
+        elif o["dst"] is not None:
+            peer = T.cores[(rank + o["dst"]) % N]
+            rid, pid, _ = topo.addr(peer)
+            es = lanes(core, peer)
+            if len(args) == 3:
+                g.remote_dma_fused([RemoteDMATransfer(
+                    dst_ids=[DstId(rid=rid, pnc=pid)], dma_engine_mask=bits(es), remote_sem=T.sem[o["sem"]],
+                    srcs=args[1:], dsts=args[:1], alu_op=1)], local_sem=T.sem.sent)
+            else:
+                g.remote_dma(args[0], args[1], T.sem[o["sem"]], T.sem.sent, pid, rid, bits(es))
+            sent += len(es)
+        elif o["sem"] is not None:
+            q.dma_start(args[0], args[1], **o["kw"]).then_inc(T.sem[o["sem"]], 16)
+        else:
+            ins = calls[o["fn"]](*args, **{a: view(b) for a, b in o["kw"].items()})
+            if o.get("mark"):
+                ins.then_inc(T.sem["s" + o["eng"]], 1)
+    g.wait_ge(T.sem.sent, sent)
+    for o in OPS:
+        if o["sem"] is not None and o["dst"] is None and not o.get("mark"):
+            g.sync.wait_ge(T.sem[o["sem"]], 16)

@@ -6,20 +6,30 @@ AT, BT = (13, 12, 14), (11, 9, 10)
 S = S0 + C * NT
 HALF = 1536
 BIG = 4096.0
-FO = 3200
+H = 65536.0
+FN = 3376
+WS = 35
+PAD = 16
 
-NB = {"s0": 12, "s1": 12, "s2": 8, "d01": 12, "d02": 8, "d12": 8}
-FGS = 1
-DMAE = ("s0", "s1", "s2", "d02")
+NB = {"s0": 16, "s1": 10, "s2": 8, "d01": 16, "d02": 12, "d12": 8}
+REP = {"s0": 2, "s1": 2, "s2": 2, "d01": 4, "d02": 2, "d12": 4}
+SINGLE = {"s0": 0, "s1": 8, "s2": 4, "d01": 0, "d02": 0, "d12": 0}
+ONS = "LV2 LV1 xls2 xed01 xed02 xed12 gn2 Wn1 Wn0 LV0 LV2d xld12 hb0".split()
+FT = "F0 F0 F0".split()
+FIRST = {"s0": 2, "s1": 0, "s2": 0, "d01": 0, "d02": 0, "d12": 0}
+GR = 2
+FGS = (2, 2, 1)
 NCH = 4
-LAGM, LAGE = 0, 0
-GCH = 32
-CY, CP, GA, SC = 1.04, 0.55, 1.56, 3.8
-LAT, LATS, HOP, ISSUE, XLAT = 110.0, 70.0, 2600.0, 700.0, 16000.0
-WIN, SLACK, MARGIN = 60.0, 400.0, 2500.0
-OFF = {"ms0": 6, "s0": 13, "s1": 3, "s2": 2, "md01": 6, "ms1": 5, "md12": 19, "p": 7, "r1": -2, "ed02": -2,
-       "ed01": -4, "es0": 9, "ms2": 5, "c": 5, "r2": -14, "ed12": 1}
-POOLS = {"cnt": [0, 1], "dif": [3, 4, 2], "xlp": [5], "log": [6, 7]}
+FCH = 422
+P = {"cy": 1.04, "cp": 0.55, "ga": 1.56, "sc": 3.8, "v0": 40.0, "s0": 80.0, "vi": 60.0, "lat": 110.0, "lats": 70.0,
+     "hop": 2600.0, "issue": 700.0, "xlat": 16000.0, "dma": 2000.0, "bw": 190.0}
+WIN = 30.0
+SLACK = 450.0
+AHEAD = 2000.0
+RANK = "s0 md12 ms0 s2 dif ms1 es0 md01 p r0 s1 es1 r2 ed01 ms2 r1 f md02 rest ed02 es2 ed12 c f1".split()
+RANK2 = "ms0 p s2 r0 ms1 es1 ms2 s1 md12 md01 s0 c f1 es0 r2 r1 ed12 md02 ed01 es2 f ed02".split()
+URGENT = "s0 s1 ed12 ed02 c f ms2 md01 md12 es2 ms0".split()
+POOLS = {"dif": [0, 1], "cnt": [2, 3, 4], "hld": [5], "log": [6, 7]}
 
 JOBS = {
     "s0": (0, S0, "Qs", "Qs", 0, "xw"), "s1": (1, S0, "Qs1", "Qs1", 0, "xw"), "s2": (2, S0, "Qs", "Qs", 0, "xw2"),
@@ -36,41 +46,49 @@ def _decl(names, cols, dtype):
 
 _decl("xw xw2", V + 16, "bfloat16")
 _decl("mi", 2 * S0, "int32")
-_decl("U E LR YM YI", S, "float32")
-_decl("F", 2 * FO, "float32")
+_decl("M", PAD + S, "float32")
+_decl("EA", PAD + S0 + C, "float32")
+_decl("E LR YM YI", S, "float32")
+_decl(" ".join(sorted(set(FT))), FN, "float32")
 _decl("Qs Qs1", 2 * S0 + 16, "uint16")
-_decl("Qm0 Qm1 Qm01", 136, "uint16")
-_decl("Qe0 Qe1 Qe01 EG", C, "uint16")
-for _t in range(NT):
-    _decl("TW%d" % _t, S0 + C * _t + C, "bfloat16")
-    _decl("TD%d" % _t, S0 + C * _t, "bfloat16")
+_decl("Qm0 Qm1 Qm01", C + 6, "uint16")
+_decl("Qe0 Qe1 Qe01", C, "uint16")
+_decl("LV", S, "bfloat16")
+_decl("TD0 TD1 TD2", S0 + 2 * C, "bfloat16")
 for _j, _v in JOBS.items():
-    _decl("xl_%s" % _j, _v[1], "bfloat16")
+    _decl("xl_%s" % _j, REP[_j] * _v[1], "bfloat16")
     _decl("cm_%s ce_%s xe_%s" % (_j, _j, _j), 16 * _v[1], "bfloat16")
     if _v[0] == 1:
         _decl("am_%s ae_%s" % (_j, _j), _v[1], "bfloat16")
-_decl("G2 Z2", 2 * S0, "float32")
-_decl("W DG SG cap rm R R16", S0, "float32")
-_decl("gcb", S0 + 2 * C, "bfloat16")
-_decl("AS AB", S0, "bfloat16")
-_decl("hb", 32, "bfloat16")
-_decl("junk", 192, "bfloat16")
-_decl("bc cumT zero", 32, "float32")
-_decl("fine C96", C, "bfloat16")
-_decl("acc tq tt s1 Kc Kb", 8, "float32")
+_decl("ZM ZE", 2 * S0 + 32, "float32")
+_decl("ZD", 2 * C + 32, "float32")
+_decl("GO", C + 2 * PAD, "float32")
+_decl("W DG", S0, "float32")
+_decl("R16 off rm", S0, "bfloat16")
+_decl("N0 Mb", S0 + C, "bfloat16")
+_decl("ASm ASe ABm ABe TM", S0 // 2, "bfloat16")
+_decl("AM fine C96 old", C, "bfloat16")
+_decl("RK", C, "float32")
+_decl("hb", 48, "bfloat16")
+_decl("cz", 48, "float32")
+_decl("z al IDX", 6 * WS, "bfloat16")
+_decl("TS IX", 6 * WS, "float32")
 _decl("ids ll", 8 * NT, "uint16")
-_decl("al permd", 8, "uint16")
-_decl("ug lg ls sm eg", C, "float32")
-_decl("GO stay LG sl", C * NT, "float32")
-_decl("FG", 16 * C, "float16")
-_decl("I NI BO SU", 128, "bfloat16")
-_decl("BO32 MT M4", 128, "float32")
-_decl("B", 144, "bfloat16")
-_decl("Bh", 144, "float16")
-_decl("PI", 8, "int32")
-_decl("PF CB low", 16, "float32")
-_decl("dup", 32, "uint16")
+_decl("EG", C * NT, "uint16")
+_decl("LG", C * NT, "float16")
+_decl("gp gn df", C * NT, "bfloat16")
+_decl("stay kept", C * NT, "float32")
+_decl("FG", 16 * C * NT, "float16")
+_decl("ali permd", 8, "uint16")
 _decl("perm", 16, "uint16")
+_decl("I NI IK BO SU MT", 128, "bfloat16")
+_decl("BO32 NI32", 128, "float32")
+_decl("R", 144, "float32")
+_decl("B BN", 144, "bfloat16")
+_decl("Bh", 144, "float16")
+_decl("PI KI", 8, "int32")
+_decl("PF CB low", 16, "float32")
+_decl("Kc K1 K2 K3", 8, "float32")
 
 SCRATCH = {"b_" + nm: ("sbuf", [128, c], d) for nm, (c, d) in BUF.items()}
 for _b in range(8):
@@ -87,6 +105,10 @@ def A(name, a=0, b=None, s=1):
 
 def IND(win, off):
     return ("ind", win, off)
+
+
+def MM(a, b):
+    return A("M", PAD + a, PAD + b)
 
 
 def _isap(x):
@@ -126,10 +148,10 @@ def op(eng, fn, outs, ins, args, cost, kw=None, lat=0.0, sem=None, dst=None):
 
 def _vcost(out, in0, per):
     if out[0] == "ind":
-        return 60 + SC * _n(out) * CY
+        return P["vi"] + P["sc"] * _n(out) * P["cy"]
     if in0[0] == "ind":
-        return 60 + GA * _n(out) * CY
-    return 40 + max(64, per * _n(in0)) * CY
+        return P["vi"] + P["ga"] * _n(out) * P["cy"]
+    return P["v0"] + max(64, per * _n(in0)) * P["cy"]
 
 
 def tt(out, a, b, o):
@@ -150,35 +172,54 @@ def ms(out, c):
 
 
 def scan(out, d0, d1, init, o0, o1):
-    op("v", "tensor_tensor_scan", [out], [d0, d1], [out, d0, d1, init, o0, o1], _vcost(out, d0, 1))
+    two = _two(out) and _two(d0) and _two(d1)
+    op("v", "tensor_tensor_scan", [out], [d0, d1], [out, d0, d1, init, o0, o1], _vcost(out, d0, 0.5 if two else 1))
 
 
-def vtranspose(n):
-    op("v", "transpose", [A("Z2", 0, n)], [A("G2", 0, n)], [A("Z2", 0, n), A("G2", 0, n)], 40 + n * CY)
+def vtranspose(out, a):
+    op("v", "transpose", [out], [a], [out, a], _vcost(out, a, 1))
 
 
-def act(out, a, f, bias=0.0, scale=1.0, accum=None):
+def act(out, a, f, bias=0.0, scale=1.0):
     kw = {} if f == ACT.Copy else {"bias": bias, "scale": scale}
-    outs = [out]
-    if accum is not None:
-        kw["accum_out"] = accum
-        outs.append(accum)
-    cost = 80 + GA * _n(out) * CY if a[0] == "ind" else 80 + max(64, _n(out)) * CY
-    op("s", "activation", outs, [a, bias, scale], [out, a, f], cost, kw)
+    cost = P["s0"] + (P["ga"] * _n(out) if a[0] == "ind" else max(64, _n(out))) * P["cy"]
+    op("s", "activation", [out], [a, bias, scale], [out, a, f], cost, kw)
+
+
+def relu(out, a, bias, name):
+    if name in ONS:
+        act(out, a, ACT.Relu, bias)
+    else:
+        ts(out, a, bias, 0.0, ALU.add, ALU.max)
+
+
+def gather(out, a, name):
+    if name in ONS:
+        act(out, a, ACT.Copy)
+    else:
+        cp(out, a)
+
+
+def after(name):
+    OPS[-1]["after"] = [k for k, x in enumerate(OPS[:-1]) if x["wr"] and x["wr"][0][0] == name][-1]
 
 
 def mm(out, l, r, start, stop):
     four = 4 if BUF[r[1]][1] == "float32" else 1
-    op("p", "matmul", [out], [l, r], [out, l, r, start, stop], 10 + four * max(64, _n(r)) * CP)
+    op("p", "matmul", [out], [l, r], [out, l, r, start, stop], 10 + four * max(64, _n(r)) * P["cp"])
 
 
 def iota(out, pat, base, cm):
     kw = {} if BUF[out[1]][1] == "int32" else {"allow_small_or_imprecise_dtypes": True}
-    op("g", "iota", [out], [], [out, pat, base, cm], 160 + 2 * _n(out) * CY, kw)
+    op("g", "iota", [out], [], [out, pat, base, cm], (156 + 2 * _n(out)) * P["cy"], kw)
 
 
-def aff(out, a, pat, cmp_op, fill, base, cm):
-    op("g", "affine_select", [out], [a], [out, a, pat, cmp_op, fill, base, cm], 210 + 2 * _n(out) * CY)
+def fill(out, c):
+    iota(out, [[0, _n(out)]], int(c), 0)
+
+
+def aff(out, a, pat, cmp_op, c, base, cm):
+    op("g", "affine_select", [out], [a], [out, a, pat, cmp_op, c, base, cm], (205 + 2 * _n(out)) * P["cy"])
 
 
 def dma(eng, out, a, nbytes, add=False):
@@ -187,16 +228,17 @@ def dma(eng, out, a, nbytes, add=False):
     outs = [out] if out[1] in BUF else []
     ins = [a] if a[1] in BUF else []
     if add:
-        op(eng, "dma_start", outs, ins + outs, [out, a], ISSUE, {"accum_op": ALU.add}, 2200 + nbytes / 95.0, sem)
+        op(eng, "dma_start", outs, ins + outs, [out, a], P["issue"], {"accum_op": ALU.add},
+           P["dma"] + 200 + 2 * nbytes / P["bw"], sem)
     else:
-        op(eng, "dma_start", outs, ins, [out, a], 80.0, lat=2000 + nbytes / 190.0, sem=sem)
+        op(eng, "dma_start", outs, ins, [out, a], P["issue"] if eng == "g" else 80.0, lat=P["dma"] + nbytes / P["bw"], sem=sem)
 
 
-def send(dst, out, a, a2=None):
+def send(dst, out, *srcs):
     sem = "r%d" % len(SEMS)
     SEMS.append(sem)
-    op("g", "remote_dma", [out], [a, a2], [out, a] + ([] if a2 is None else [a2]), ISSUE,
-       lat=HOP + 256 * _n(a) / 60.0, sem=sem, dst=dst)
+    op("g", "remote_dma", [out], list(srcs), [out] + list(srcs), P["issue"],
+       lat=P["hop"] + 256 * _n(out) / 60.0, sem=sem, dst=dst)
 
 
 def col(name, c):
@@ -207,171 +249,226 @@ def sel(name, i):
     return A(name, 15 - i, 143 - i)
 
 
+def per(name, t):
+    w = BUF[name][0] // NT
+    return A(name, w * t, w * t + (6 if w == 8 else w))
+
+
 BIASCOL = {}
 
 
 def constants():
     iota(col("PI", 0), [[0, 1]], 0, 1)
-    ms(A("M4"), -BIG)
-    aff(A("M4"), A("M4"), [[-16, 8], [0, 16]], ALU.is_ge, 0.0, 0, 1)
-    aff(A("M4"), A("M4"), [[16, 8], [0, 16]], ALU.is_ge, 0.0, 15, -1)
-    aff(A("MT"), A("M4"), [[1, 128]], ALU.is_gt, 0.0, 0, -1)
-    aff(A("MT"), A("MT"), [[1, 128]], ALU.not_equal, 1.0, 0, -1)
-    iota(A("R"), [[1, S0]], 0, 0)
-    iota(A("R16"), [[0, 16], [1, 16]], 0, 0)
-    for c, m in ((1, 15), (2, 112), (3, 16), (4, 7)):
-        ts(col("PI", c), col("PI", 0), m, None, ALU.bitwise_and)
-    ts(col("PI", 5), col("PI", 0), 3, 1, ALU.logical_shift_right, ALU.bitwise_and)
-    cp(A("PF", 0, 6), A("PI", 0, 6))
-    pb, pg, pc = col("PF", 1), col("PF", 2), col("PF", 3)
-    ts(col("PF", 6), pb, 32.0, pc, ALU.mult, ALU.add)
-    ts(col("PF", 7), col("PF", 4), 5.0, 32.0, ALU.min, ALU.mult)
-    ts(col("PF", 8), col("PF", 7), pc, col("PF", 5), ALU.add, ALU.add)
-    ts(A("dup", 0, 32, 2), A("R", 0, S0, 16), pb, None, ALU.add)
-    ts(A("dup", 1, 32, 2), A("R", 0, S0, 16), pb, None, ALU.add)
-    ts(A("perm"), A("R", 0, 16), col("PF", 6), None, ALU.add)
-    ts(A("permd"), A("R", 0, 16, 2), col("PF", 8), None, ALU.add)
-    act(A("BO32"), A("M4"), ACT.Identity, 0.0, -1.0 / BIG)
-    act(A("BO"), A("M4"), ACT.Identity, 0.0, -1.0 / BIG)
-    aff(A("SU"), A("BO"), [[-1, 128]], ALU.is_gt, 0.0, 0, 1)
-    ms(A("zero"), 0.0)
-    ms(A("cumT"), 65536.0)
-    ts(A("B"), A("R", 0, 144), pg, 15.0, ALU.subtract, ALU.is_equal)
-    ts(A("Bh"), A("B"), 1.0 / 16, None, ALU.mult)
+    iota(col("PI", 4), [[0, 1]], 0, 17)
+    fill(A("BO32"), 1)
+    aff(A("BO32"), A("BO32"), [[-16, 8], [0, 16]], ALU.is_ge, 0.0, 0, 1)
+    aff(A("BO32"), A("BO32"), [[16, 8], [0, 16]], ALU.is_ge, 0.0, 15, -1)
+    aff(A("MT"), A("BO32"), [[1, 128]], ALU.is_gt, 0.0, 0, -1)
+    aff(A("SU"), A("BO32"), [[-1, 128]], ALU.is_gt, 0.0, 0, 1)
+    iota(A("R"), [[1, 144]], 0, 0)
+    ts(col("PI", 1), col("PI", 0), 15, None, ALU.bitwise_and)
+    ts(col("PI", 2), col("PI", 0), 112, None, ALU.bitwise_and)
+    ts(col("PI", 3), col("PI", 4), 4, 1, ALU.logical_shift_right, ALU.bitwise_and)
+    cp(A("PF", 0, 4), A("PI", 0, 4))
+    pb, pg, odd = col("PF", 1), col("PF", 2), col("PF", 3)
     ts(A("I"), A("R", 0, 128), col("PF", 0), None, ALU.is_equal)
+    ts(A("B"), A("R"), pg, 15.0, ALU.subtract, ALU.is_equal)
+    act(A("NI32"), A("I"), ACT.Identity, 0.0, -1.0)
     act(A("NI"), A("I"), ACT.Identity, 0.0, -1.0)
-    ts(A("cap"), A("R16"), pb, None, ALU.is_equal)
-    act(A("W"), A("R"), ACT.Identity, float(V + 1))
-    tt(A("cap"), A("cap"), A("W"), ALU.mult)
-    act(A("rm"), A("R16"), ACT.Sign)
+    act(A("IK"), A("I"), ACT.Identity, 0.0, BIG)
+    act(A("BN"), A("B"), ACT.Identity, 0.0, -BIG)
+    act(A("Bh"), A("B"), ACT.Identity, 0.0, 1.0 / 16)
+    act(A("BO"), A("BO32"), ACT.Copy)
+    act(col("PF", 4), odd, ACT.Identity, 0.0, float(S0 + 16))
+    act(col("PF", 5), pb, ACT.Identity, col("PF", 4), 16.0)
+    ts(A("perm"), A("R", 0, 16), col("PF", 5), None, ALU.add)
     act(A("Kc", 0, 6), A("R", 0, C, 16), ACT.Identity, pb)
-    act(A("Kb", 0, 6), A("Kc", 0, 6), ACT.Identity, 0.5)
-    ms(A("C96"), HALF / 16.0)
+    ts(A("K1", 0, 6), A("Kc", 0, 6), -2.5, 1.0 / 6, ALU.add, ALU.mult)
+    cp(A("KI", 0, 6), A("K1", 0, 6))
+    act(col("PF", 6), odd, ACT.Identity, 0.0, float(C + 16))
+    act(A("K2", 0, 6), A("Kc", 0, 6), ACT.Identity, col("PF", 6), 16.0)
+    ts(A("K1", 0, 6), A("KI", 0, 6), -95.0, None, ALU.mult)
+    tt(A("K3", 0, 6), A("K1", 0, 6), A("K2", 0, 6), ALU.add)
+    cp(A("permd", 0, 6), A("K3", 0, 6))
+    iota(A("R16"), [[0, 16], [1, 16]], 0, 0)
+    ts(A("off"), A("R16"), pb, -2 * BIG, ALU.not_equal, ALU.mult)
+    act(A("rm"), A("R16"), ACT.Sign)
+    fill(A("TS"), -30000)
+    act(A("TS", 0, 6 * WS, WS), A("Kc", 0, 6), ACT.Identity, 0.5)
+    iota(A("IX"), [[0, 6], [1, WS]], 0, 0)
+    act(A("IDX"), A("IX"), ACT.Identity, 0.0, 1.0 / 256)
+    act(A("RK"), A("R", 0, C), ACT.Identity, col("TS", 0), -1.0)
+    fill(A("hb", 1, WS), -1)
+    fill(col("hb", 0), 0)
+    fill(A("C96"), HALF // 16)
     ms(col("CB", 0), 2.0 ** -112)
+    act(col("CB", 1), pb, ACT.Identity, float(V), -H)
     for j, v in JOBS.items():
-        key = (NB[j], AT[v[0]])
+        key = (NB.get(j, 16), AT[v[0]], j == "s1")
         if key not in BIASCOL:
-            c = 1 + len(BIASCOL)
+            a = key[1]
+            one = 1.0 if key[2] else 0.0
+            if key[0] == 16:
+                BIASCOL[key] = 2 * BIG * (a - 8) - one
+                continue
+            c = col("CB", 2 + len(BIASCOL))
             BIASCOL[key] = c
-            ts(col("CB", c), pb, float(key[0]), 2 * BIG * (key[1] - 16), ALU.is_lt, ALU.mult)
-            act(col("CB", c), col("CB", c), ACT.Identity, 2 * BIG * key[1])
-    act(col("CB", 14), col("CB", BIASCOL[(NB["s1"], AT[1])]), ACT.Identity, 0.0, 0.5 / BIG)
+            ts(c, pb, float(key[0]), BIG * (a - 16), ALU.is_lt, ALU.mult)
+            act(c, c, ACT.Identity, BIG * a - one)
     ms(A("low"), -2.0 ** 99)
     act(A("xw", V), A("low"), ACT.Identity, 0.0, 4.0)
     act(A("xw2", V), A("low"), ACT.Identity, 0.0, 4.0)
-    ms(A("U", S0), 0.0)
-    ms(A("E", S0), 2 * BIG)
-    ms(A("LR", S0), 65536.0)
-    for t in range(NT):
-        ms(A("TW%d" % t, S0 + C * t), 0.0)
-    ms(A("Qm0", 128), 0)
-    for a in range(0, 2 * FO, 400):
-        iota(A("F", a, a + 400), [[1, 400]], a % FO - HALF, 0)
+    ms(A("M", 0, PAD), 0.0)
+    ms(MM(S0, S0 + PAD), H)
+    fill(MM(S0 + PAD, S), H)
+    ms(A("EA", 0, PAD), 0.0)
+    ms(A("EA", PAD + S0), float(V))
+    fill(A("E", S0), V)
+    fill(A("YI", S - C), V)
+    fill(A("LV", S0), 0)
+    fill(A("N0", S0), 0)
+    fill(A("TD0", S0, S0 + C), BIG)
+    fill(A("TD1", S0 + C), 0)
+    fill(A("GO", 0, PAD), 0)
+    fill(A("GO", PAD + C), 0)
+    iota(A("LR", S0), [[1, S - S0]], V + 1 - HALF, 0)
 
 
-def leaders(src, n, tag, lr, lst):
+def names():
+    for f in sorted(set(FT)):
+        TAG[0] = "f" if f == FT[0] else "f1"
+        w = FCH if f == FT[0] else FCH // 2
+        for a in range(0, FN, w):
+            iota(A(f, a, a + w), [[1, w]], a - HALF, 0)
+
+
+def leaders(src, none, n, tag, lr, lst):
     pa, pb = A("@log" + tag + "a", 0, n), A("@log" + tag + "b", 0, n)
-    mm(pa, A("MT"), src, True, True)
-    act(A("W", 0, n), pa, ACT.Relu)
-    mm(pb, A("BO32"), A("W", 0, n), True, True)
+    mm(pa, A("MT"), none, True, False)
+    mm(pa, A("NI32"), src, False, True)
+    relu(A("W", 0, n), pa, col("CB", 1), "W" + tag)
     if lst is not None:
-        tt(A("DG", 0, n), pb, A("cap", 0, n), ALU.min)
-    act(lr, pb, ACT.Identity, float(V), -1.0)
-    if lst is not None:
-        scan(A("SG", 0, n), A("rm", 0, n), A("DG", 0, n), 0.0, ALU.mult, ALU.add)
-        ts(lst, A("SG", 15, n, 16), -1.0, float(V), ALU.mult, ALU.add)
+        mm(pb, A("BO32"), A("W", 0, n), True, False)
+        mm(pb, A("I"), A("off", 0, n), False, True)
+        scan(A("DG", 0, n), A("rm", 0, n), pb, 0.0, ALU.mult, ALU.max)
+        ts(lst, A("DG", 15, n, 16), -1.0, float(V), ALU.mult, ALU.add)
+    mm(pa, A("BO32"), A("W", 0, n), True, True)
+    act(lr, pa, ACT.Identity, float(V - HALF), -1.0)
+
+
+def turn(out, src, z, n, perm):
+    vtranspose(A(z, 0, n), A(src, PAD, PAD + n))
+    vtranspose(A(z, n, 2 * n + 32), A(src, 0, n + 32))
+    ts(out, IND(A(z), perm), float(V), None, ALU.min)
 
 
 def prepare():
     dma("y", A("mi", 0, S0), ("ap", "mem0", 0, S0, 1), 131072)
     dma("s", A("mi", S0), ("ap", "inv0", 0, S0, 1), 131072)
-    dma("y", A("xw", 0, V), ("ap", "xs", 0, V, 1), 786432)
+    dma("y", A("xw", 0, V), ("ap", "xs", 0, V, 1), 786432 + 262144)
     OPS[-1]["after"] = len(OPS) - 3
-    ts(A("U", 0, S0), A("mi", 0, S0), -1.0, float(V), ALU.mult, ALU.add)
-    act(A("G2"), IND(A("U", 0, S0), A("dup")), ACT.Identity, float(V), -1.0)
-    cp(A("Qs", S0 + 16), A("mi", S0))
-    cp(A("E", 0, S0), A("mi", S0))
-    leaders(A("U", 0, S0), S0, "p", A("LR", 0, S0), A("Qs", S0, S0 + 16))
-    vtranspose(2 * S0)
-    cp(A("Qs", 0, S0), IND(A("Z2"), A("perm")))
+    ts(A("N0", 0, S0), A("mi", 0, S0), float(V), H, ALU.is_ge, ALU.mult)
+    cp(MM(0, S0), A("mi", 0, S0))
+    leaders(MM(0, S0), A("N0", 0, S0), S0, "p", A("LR", 0, S0), A("Qs", 2 * S0))
+    turn(A("Qs", 0, S0), "M", "ZM", S0, A("perm"))
+    cp(A("EA", PAD, PAD + S0), A("mi", S0))
+    turn(A("Qs", S0, 2 * S0), "EA", "ZE", S0, A("perm"))
+    dma("y", A("E", 0, S0), A("EA", PAD, PAD + S0), 131072)
     send(1, A("Qs1"), A("Qs"))
-    op("g", "relay", [A("xw2", 0, V)], [A("xw", 0, V)], [], NCH * ISSUE, lat=XLAT, sem="xa", dst=-2)
+    op("g", "relay", [A("xw2", 0, V)], [A("xw", 0, V)], [], NCH * P["issue"], lat=P["xlat"], sem="xa", dst=-2)
+
+
+def compare(j, out, q, o, rows, alu):
+    _, n, _, _, _, xw = JOBS[j]
+    k = n // 16
+    i = rows[0]
+    while i < rows[1]:
+        r = 1 if i >= 16 - SINGLE[j] or i < FIRST[j] else min(REP[j], rows[1] - i)
+        tt(A(out, i * n, (i + r) * n), IND(A(xw), A(q, o + i * k, o + (i + r) * k)), A("xl_" + j, 0, r * n), alu)
+        i += r
+
+
+def answer(out, a):
+    send(-1, A(out), A(a, 0, S0 // 2), A(a, 0, S0 // 2), A(a, S0 // 2, S0))
+
+
+def second(out, src, tmp):
+    act(A(tmp), A(src), ACT.Abs, 1.0)
+    act(out, A(tmp), ACT.Abs, -BIG, BIG / 2)
 
 
 def members(j):
     t, n, q, _, s0, xw = JOBS[j]
-    w = 16 if n == S0 else 8
-    k = n // 16
-    xl = A("xl_" + j)
-    cnt = A("@cntm" + j, 0, n)
-    act(xl, IND(A(xw), A(q, 16 * w, 16 * w + k)), ACT.Copy)
-    first = len(OPS)
+    o = 2 * S0 if n == S0 else C
+    xl = "xl_" + j
+    gather(A(xl, 0, n), IND(A(xw), A(q, o, o + n // 16)), "xl" + j)
+    for r in range(1, REP[j]):
+        if j in ("s0", "d01", "d12"):
+            gather(A(xl, r * n, (r + 1) * n), A(xl, 0, n), "xl" + j)
+        else:
+            dma("y", A(xl, r * n, (r + 1) * n), A(xl, 0, n), 256 * n)
+    compare(j, "cm_" + j, q, 0, (0, 16), ALU.is_equal)
+    held = j in ("s2", "d02")
+    cnt = A("@hld", s0, s0 + n) if held else A(("@log" if n == C else "@hld") + j, 0, n)
+    opened = held or j == "s0"
+    if j == "s0":
+        mm(cnt, A("NI"), A("N0", 0, n), True, False)
+    if j == "s2":
+        mm(A("@hld", 0, S0 + C), A("NI"), A("N0"), True, False)
+        after("@hldl")
     for i in range(16):
-        tt(A("cm_" + j, i * n, (i + 1) * n), IND(A(xw), A(q, i * w, i * w + k)), xl, ALU.is_equal)
-    for i in range(16):
-        mm(cnt, sel("B", i), A("cm_" + j, i * n, (i + 1) * n), i == 0, i == 15)
-        OPS[-1]["after"] = first + min(15, i + LAGM)
-    home = A("TW%d" % t, s0, s0 + n)
-    if j == "s1":
-        ts(A("am_" + j), cnt, float(BT[t]), 2 * BIG, ALU.is_lt, ALU.mult)
-        return
-    act(A("am_" + j) if t == 1 else home, cnt, ACT.Relu, BIG * BT[t], -BIG)
-    if t == 1:
-        send(-1, home, A("am_" + j))
+        mm(cnt, sel("BN", i), A("cm_" + j, i * n, (i + 1) * n), i == 0 and not opened, i == 15 and t < 2)
+    if j == "s0":
+        relu(A("LV", 0, n), cnt, BIG * BT[t], "LV0")
+    elif j == "s1":
+        act(A("am_s1"), cnt, ACT.Sign, BIG * BT[t] - 1.0)
+        answer("ASm", "am_s1")
+    elif j == "d01":
+        relu(A("am_d01"), cnt, BIG * BT[t], "am")
+        send(-1, A("AM"), A("am_d01"))
 
 
 def bounds(j):
     t, n, _, q, s0, xw = JOBS[j]
-    o = S0 + 16 if n == S0 else 0
-    xl = A("xl_" + j)
+    xl, xe, ce = "xl_" + j, "xe_" + j, "ce_" + j
     cnt = A("@cnte" + j, 0, n)
-    ch = GCH if n == S0 else C // 2
-    for a in range(0, n, ch):
-        act(A("xe_" + j, 16 * a, 16 * (a + ch)), IND(A(xw), A(q, o + a, o + a + ch)), ACT.Copy)
-    nb = NB[j]
-    per_bank = 2 if n == S0 else 4
-    units = [("b", list(range(i, min(nb, i + per_bank)))) for i in range(0, nb, per_bank)]
-    cs = list(range(nb, 16))
-    seq = []
-    while units or cs:
-        if units:
-            seq.append(units.pop(0))
-        if cs:
-            seq.append(("c", [cs.pop(0)]))
-    if nb < 16:
-        mm(A("@xlp" + j, 0, n), A("I"), xl, True, True)
-    made = []
-    for kind, rows in seq:
-        if kind == "b":
-            bank = "@dif%s_%d" % (j, rows[0])
-            for z, i in enumerate(rows):
-                mm(A(bank, z * n, (z + 1) * n), A("I"), A("xe_" + j, i, 16 * n, 16), True, False)
-                mm(A(bank, z * n, (z + 1) * n), A("NI"), xl, False, True)
-            act(A("ce_" + j, rows[0] * n, (rows[-1] + 1) * n), A(bank, 0, len(rows) * n), ACT.Sign, col("CB", 0))
-        else:
-            i = rows[0]
-            tt(A("ce_" + j, i * n, (i + 1) * n), A("xe_" + j, i, 16 * n, 16), A("@xlp" + j, 0, n), ALU.is_ge)
-        made += [(i, len(OPS) - 1) for i in rows]
-    for z, (i, _) in enumerate(made):
-        mm(cnt, sel("B", i), A("ce_" + j, i * n, (i + 1) * n), z == 0, z == 15)
-        OPS[-1]["after"] = made[min(15, z + LAGE)][1]
+    nb = NB.get(j, 16)
+    if n == S0:
+        for i in range(0, nb, GR):
+            e = min(nb, i + GR)
+            act(A(xe, i * n, e * n), IND(A(xw), A(q, S0 + 16 * i, S0 + 16 * e)), ACT.Copy)
+        for i in range(0, nb, 2):
+            w = min(2, nb - i) * n
+            bank = A("@dif%s_%d" % (j, i), 0, w)
+            mm(bank, A("I"), A(xe, i * n, i * n + w), True, False)
+            mm(bank, A("NI"), A(xl, 0, w), False, True)
+            act(A(ce, i * n, i * n + w), bank, ACT.Sign, col("CB", 0))
+        compare(j, ce, q, S0, (nb, 16), ALU.is_ge)
+    else:
+        act(A(xe, 0, 8 * C), IND(A(xw), A(q, 0, C // 2)), ACT.Copy)
+        gather(A(xe, 8 * C), IND(A(xw), A(q, C // 2)), "xe" + j)
+        for i in range(0, nb, 4):
+            bank = "@dif%s_%d" % (j, i)
+            for z in range(4):
+                mm(A(bank, z * n, (z + 1) * n), A("I"), A(xe, i + z, 16 * n, 16), True, False)
+                mm(A(bank, z * n, (z + 1) * n), A("NI"), A(xl, 0, n), False, True)
+            act(A(ce, i * n, (i + 4) * n), A(bank, 0, 4 * n), ACT.Sign, col("CB", 0))
+        if nb < 16:
+            mm(A("@difx" + j, 0, n), A("I"), A(xl, 0, n), True, True)
+        for i in range(nb, 16):
+            tt(A(ce, i * n, (i + 1) * n), A(xe, i, 16 * n, 16), A("@difx" + j, 0, n), ALU.is_ge)
+    for i in range(16):
+        mm(cnt, sel("BN", i), A(ce, i * n, (i + 1) * n), i == 0, i == 15)
+    bias = BIASCOL[(nb, AT[t], j == "s1")]
     home = A("TD%d" % t, s0, s0 + n)
     if j == "s1":
-        ts(A("ae_" + j), cnt, col("CB", 14), -BIG, ALU.is_ge, ALU.mult)
-        send(-1, A("AS"), A("am_" + j), A("ae_" + j))
-        return
-    act(A("ae_" + j) if t == 1 else home, cnt, ACT.Relu, col("CB", BIASCOL[(nb, AT[t])]), -2 * BIG)
-    if t == 1:
-        send(-1, home, A("ae_" + j))
-
-
-def parts(t):
-    return [(0, S0)] + [(S0 + C * z, S0 + C * (z + 1)) for z in range(t)]
-
-
-def per(name, t):
-    w = BUF[name][0] // NT
-    return A(name, w * t, w * t + (6 if w == 8 else w))
+        act(A("ae_s1"), cnt, ACT.Sign, bias)
+        answer("ASe", "ae_s1")
+    elif j == "d01":
+        act(A("ae_d01"), cnt, ACT.Relu, bias)
+        send(-1, home, A("ae_d01"))
+    else:
+        act(home, cnt, ACT.Relu, bias)
 
 
 def positions(t):
@@ -379,107 +476,133 @@ def positions(t):
     na = n // 16
     h, u, f = A("@logh%d" % t, 0, na), "@logu%d" % t, A("@logi%d" % t, 0, 6)
     for b in range(16):
-        mm(h, sel("B", b), A("gcb", b, n, 16), b == 0, b == 15)
-    act(A("hb", 0, na), h, ACT.Sign)
-    mm(A(u, 0, na), A("BO"), A("hb", 0, na), True, True)
-    mm(A(u, 32, 32 + na), A("SU"), A("hb", 0, na), True, True)
-    bc = A("bc", 0, na)
-    scan(bc, A(u, 0, na), A("zero", 0, na), 0.0, ALU.add, ALU.add)
-    tt(A("cumT", 0, na), bc, A(u, 32, 32 + na), ALU.subtract)
-    for a in range(6):
-        act(A("junk", 32 * a, 32 * a + na), bc, ACT.Sign, col("Kb", a), -1.0, col("acc", a))
-    ts(A("al", 0, 6), A("acc", 0, 6), 0.5, na / 2.0, ALU.mult, ALU.add)
-    tt(A("fine"), IND(A("cumT"), A("al", 0, 6)), A("R", 0, C), ALU.is_le)
-    ts(A("tq", 0, 6), A("Kc", 0, 6), col("bc", na - 1), 0.0, ALU.subtract, ALU.max)
-    act(A("tt", 0, 6), A("acc", 0, 6), ACT.Identity, 8.0 * na, 8.0)
-    tt(A("tq", 0, 6), A("tq", 0, 6), A("tt", 0, 6), ALU.add)
+        mm(h, sel("BN", b), A("LV", b, n, 16), b == 0, b == 15)
+    if "hb%d" % t in ONS:
+        act(A("hb", 1, 1 + na), h, ACT.Sign)
+    else:
+        ts(A("hb", 1, 1 + na), h, -1.0, None, ALU.max)
+    for c in range(6):
+        mm(A(u, WS * c, WS * (c + 1)), A("BO"), A("hb", 0, WS), True, True)
+    mm(A(u, 256, 256 + WS - 1), A("SU"), A("hb", 1, WS), True, True)
+    scan(A("z"), A(u, 0, 6 * WS), A("TS"), 0.0, ALU.add, ALU.max)
+    scan(A("al"), A("z"), A("IDX"), 0.0, ALU.max, ALU.min)
+    last = A("al", WS - 1, 6 * WS, WS)
+    ts(A("ali", 0, 6), last, 256.0, None, ALU.mult)
+    tt(A("cz", 0, WS - 1), A("z", 1, WS), A(u, 256, 256 + WS - 1), ALU.subtract)
+    tt(A("fine"), IND(A("cz", 0, WS - 1), A("ali", 0, 6)), A("RK"), ALU.is_ge)
     for b in range(16):
-        mm(f, sel("B", b), A("fine", b, C, 16), b == 0, b == 15)
-    tt(A("s1", 0, 6), f, A("tq", 0, 6), ALU.add)
-    cp(per("ids", t), A("s1", 0, 6))
+        mm(f, sel("B", b), A("fine", b, C, 16), b == 0, False)
+    mm(f, A("IK"), last, False, True)
+    cp(per("ids", t), f)
+
+
+def leavers(t):
+    if t == 1:
+        h = S0 // 2
+        second(A("TM"), "ASm", "ABm")
+        dma("g", A("Mb", 0, S0), MM(0, S0), 65536)
+        mm(A("@hldl", 0, S0), A("NI"), A("Mb", 0, S0), True, False)
+        after("am_s1")
+        mm(A("@hldl", 0, S0), A("NI"), A("N0", 0, S0), False, False)
+        mm(A("@hldl", 0, h), A("IK"), A("ASm"), False, False)
+        mm(A("@hldl", h, S0), A("I"), A("TM"), False, True)
+        relu(A("LV", 0, S0), A("@hldl", 0, S0), 0.0, "LV1")
+        tt(A("LV", S0, S0 + C), A("AM"), per("gn", 0), ALU.is_gt)
+    if t == 2:
+        dma("g", A("Mb"), MM(0, S0 + C), 90112)
+        mm(A("@hld", 0, S0 + C), A("NI"), A("Mb"), False, True)
+        relu(A("LV", 0, S0 + C), A("@hld", 0, S0 + C), BIG * BT[t], "LV2")
+        mm(A("@logd12", 0, C), A("NI"), per("gn", 1), False, True)
+        relu(A("LV", S0 + C, S0 + 2 * C), A("@logd12", 0, C), BIG * BT[t], "LV2d")
 
 
 def split(t):
     n = S0 + C * t
-    tw = "TW%d" % t
     last = t == NT - 1
-    ids, go, stay, sl, lg, ll = (per(x, t) for x in ("ids", "GO", "stay", "sl", "LG", "ll"))
-    if t == 1:
-        ts(A(tw, 0, S0), A("AS"), 0.0, None, ALU.max)
-    for a, b in parts(t):
-        tt(A("gcb", a, b), A(tw, a, b), A("U", a, b), ALU.min)
-    if last:
-        act(A("YM", 0, n), A("U", 0, n), ACT.Identity, float(V), -1.0)
+    ids, go, gn = per("ids", t), A("GO", PAD, PAD + C), per("gn", t)
+    leavers(t)
     positions(t)
-    cp(A("ug"), IND(A("U", 0, n + C), ids))
-    tt(go, IND(A(tw), ids), A("ug"), ALU.min)
+    if "gn%d" % t in ONS:
+        act(gn, IND(A("LV", 0, n + C), ids), ACT.Relu, H, -H)
+    else:
+        ts(gn, IND(A("LV", 0, n + C), ids), 0.0, H, ALU.is_le, ALU.mult)
+    tt(go, IND(MM(0, n + C), ids), gn, ALU.add)
+    act(per("LG", t), IND(A("LR", 0, n + C), ids), ACT.Copy)
+    leaders(go, gn, C, "n%d" % t, A("LR", n, n + C), None if last else A("Qm%d" % t, C))
     if not last:
-        act(A("G2", 0, 2 * C), IND(go, A("dup", 0, 12)), ACT.Identity, float(V), -1.0)
-    leaders(go, C, "n%d" % t, sl, None if last else A("Qm%d" % t, 128, 134))
-    if not last:
-        vtranspose(2 * C)
-        cp(A("Qm%d" % t, 0, 128), IND(A("Z2", 0, 2 * C), A("permd")))
+        turn(A("Qm%d" % t, 0, C), "GO", "ZD", C, A("permd", 0, 6))
     if t == 0:
         send(1, A("Qm01"), A("Qm0"))
-    tt(stay, A("ug"), go, ALU.subtract)
+    act(per("gp", t), gn, ACT.Identity, H, -1.0)
+    tt(per("stay", t), IND(MM(0, n + C), ids), per("gp", t), ALU.add)
+    cp(IND(MM(0, n + C), ids), per("stay", t))
     if last:
-        ts(IND(A("YM"), ids), stay, -1.0, float(V), ALU.mult, ALU.add)
-        act(A("YM", n, n + C), go, ACT.Identity, float(V), -1.0)
+        ts(A("YM", 0, n), MM(0, n), float(V), None, ALU.min)
+        ts(A("YM", n, S), go, float(V), None, ALU.min)
         dma("y", ("ap", "ym", 0, S, 1), A("YM"), 278528)
     else:
-        cp(IND(A("U", 0, n + C), ids), stay)
-        act(A("U", n, n + C), go, ACT.Copy)
-    tt(A("lg"), IND(A("LR", 0, n + C), ids), A("cap", 0, C), ALU.min)
-    if not last:
-        act(lg, IND(A("LR", 0, n + C), ids), ACT.Copy)
-        act(A("LR", n, n + C), sl, ACT.Copy)
-    scan(A("ls"), A("rm", 0, C), A("lg"), 0.0, ALU.mult, ALU.add)
-    cp(ll, A("ls", 15, C, 16))
+        dma("y", MM(n, n + C), go, 49152)
+    bank = A("@logl%d" % t, 0, 6)
+    for b in range(16):
+        mm(bank, sel("Bh", b), A("LG", C * t + b, C * (t + 1), 16), b == 0, b == 15)
+    ts(per("ll", t), bank, float(HALF), None, ALU.add)
+
+
+def deaths(t):
+    if t == 1:
+        act(A("TD1", 0, S0 // 2), A("ASe"), ACT.Relu, 0.0, BIG)
+        second(A("TD1", S0 // 2, S0), "ASe", "ABe")
+    if t == 2:
+        for a, b in ((0, S0), (S0, S0 + C), (S0 + C, S0 + 2 * C)):
+            bank = A("@cnty%d" % a, 0, b - a)
+            mm(bank, A("NI"), A("TD2", a, b), True, False)
+            mm(bank, A("NI32"), A("E", a, b), False, True)
+            ts(A("YI", a, b), bank, -1.0, float(V), ALU.mult, ALU.min)
 
 
 def rename(t):
     n = S0 + C * t
     last = t == NT - 1
-    ids, stay, sl, lg, ll = (per(x, t) for x in ("ids", "stay", "sl", "LG", "ll"))
-    ts(IND(A("F", 0, FO), ll), sl, 1.0, float(-HALF), ALU.mult, ALU.add)
-    for a, b in parts(t):
-        if t == 1 and a == 0:
-            act(A("AB"), A("AS"), ACT.Abs)
-            act(A("TD1", 0, S0), A("AB"), ACT.Abs, -2 * BIG, 2.0)
-        if any(v[0] == t and v[4] == a for j, v in JOBS.items() if j in DMAE):
-            dma("g", A("E", a, b), A("TD%d" % t, a, b), 512 * (b - a), True)
-        else:
-            tt(A("E", a, b), A("TD%d" % t, a, b), A("E", a, b), ALU.max)
-    act(A("sm"), stay, ACT.Identity, float(V + FO), -1.0)
-    tt(A("eg"), IND(A("E", 0, n + C), ids), A("sm"), ALU.min)
-    cp(A("EG"), A("eg"))
-    if last:
-        ts(A("YI", 0, n), A("E", 0, n), float(V), None, ALU.min)
-        dma("y", ("ap", "yi", 0, n, 1), A("YI", 0, n), 229376)
+    ids, ll, f, df, kept = per("ids", t), per("ll", t), FT[t], per("df", t), per("kept", t)
+    cp(IND(A(f), ll), A("LR", n, n + C))
+    ts(per("EG", t), IND(A("EA", PAD) if t == 0 else A("E", 0, n + C), ids), float(V), None, ALU.min)
+    if t == 1:
+        ts(A("old"), IND(A("E", 0, n + C), ids), float(V), float(V), ALU.is_ge, ALU.mult)
+    deaths(t)
     h = C // 2
-    for a in (0, h):
-        if a < FGS * h:
-            act(A("FG", 16 * a, 16 * (a + h)), IND(A("F"), A("EG", a, a + h)), ACT.Copy)
+    for z, a in enumerate((C * t, C * t + h)):
+        if z < FGS[t]:
+            act(A("FG", 16 * a, 16 * (a + h)), IND(A(f), A("EG", a, a + h)), ACT.Copy)
         else:
-            cp(A("FG", 16 * a, 16 * (a + h)), IND(A("F"), A("EG", a, a + h)))
+            cp(A("FG", 16 * a, 16 * (a + h)), IND(A(f), A("EG", a, a + h)))
+    if f in FT[t + 1:]:
+        cp(IND(A(f), ll), per("LG", t))
+    if t == 1:
+        tt(df, IND(A("TD1"), ids), A("old"), ALU.max)
+    else:
+        ts(df, IND(A("YI") if last else A("TD0", 0, n + C), ids), float(V), float(V), ALU.is_ge, ALU.mult)
+    if not last:
+        dma("g", A("E", 0, n), A("TD%d" % t, 0, n), 512 * n, True)
+    tt(kept, df, per("stay", t), ALU.min)
     bank = A("@logf%d" % t, 0, C)
     for i in range(16):
-        mm(bank, sel("Bh", i), A("FG", i, 16 * C, 16), i == 0, False)
-    mm(bank, A("BO"), A("C96"), False, True)
+        mm(bank, sel("Bh", i), A("FG", 16 * C * t + i, 16 * C * (t + 1), 16), i == 0, False)
+    mm(bank, A("BO"), A("C96"), False, False)
+    mm(bank, A("NI"), df, False, True)
     if last:
-        act(A("YI", n, n + C), bank, ACT.Copy)
-        dma("y", ("ap", "yi", n, S, 1), A("YI", n, S), 49152)
+        dma("y", ("ap", "yi", 0, n, 1), A("YI", 0, n), 229376)
+        tt(A("YI", n, S), bank, kept, ALU.max)
+        dma("s", ("ap", "yi", n, S, 1), A("YI", n, S), 49152)
     else:
-        cp(A("Qe%d" % t), bank)
-        act(A("E", n, n + C), bank, ACT.Copy)
+        tt(A("E", n, n + C), bank, kept, ALU.max)
+        ts(A("Qe%d" % t), A("E", n, n + C), float(V), None, ALU.min)
         if t == 0:
             send(1, A("Qe01"), A("Qe0"))
-        ts(IND(A("F", 0, FO), ll), lg, 1.0, float(-HALF), ALU.mult, ALU.add)
 
 
 def program():
-    steps = [("c", constants, None), ("p", prepare, None)]
-    for j in ("s0", "s1", "s2", 0, "d01", "d02", 1, "d12", 2):
+    steps = [("c", constants, None), ("p", prepare, None), ("f", names, None)]
+    for j in ("s0", "s1", 0, "d01", 1, "s2", "d02", "d12", 2):
         steps += [("m", members, j), ("e", bounds, j)] if j in JOBS else [("s", split, j), ("r", rename, j)]
     for tag, f, x in steps:
         TAG[0] = tag + ("" if x is None else str(x))
@@ -508,6 +631,51 @@ def dependencies():
     return {nm: [h[0] for h in v] for nm, v in hist.items() if nm[0] == "@"}
 
 
+def gap(j, k, hard):
+    if not hard:
+        return 0.0
+    return OPS[j]["lat"] + (P["lats"] if OPS[j]["eng"] == OPS[k]["eng"] else P["lat"])
+
+
+def priorities(succ):
+    n = len(OPS)
+    way = [0.0] * n
+    for k in range(n - 1, -1, -1):
+        o = OPS[k]
+        way[k] = o["cost"] + max([way[s] + gap(k, s, OPS[s]["deps"][k]) for s in succ[k]] + [o["lat"]])
+    prio = []
+    for k, o in enumerate(OPS):
+        name = o["wr"][0][0] if o["wr"] else ""
+        rank = RANK.index(o["tag"])
+        if name[:3] in ("xe_", "cm_") or name == "FG" or o["tag"][0] == "f" or (
+                name[:3] == "ce_" and o["rd"][0][0][0] != "@"):
+            prio.append((-rank, 0, -k))
+        else:
+            dif = name[:4] == "@dif"
+            prio.append((-min(rank, RANK.index("dif" if dif else "rest")), 1, -RANK2.index(o["tag"]),
+                         -k if dif else way[k]))
+    for k in range(n - 1, -1, -1):
+        if OPS[k]["tag"] == "c":
+            prio[k] = max([prio[k]] + [(prio[s][0], 3, 0, way[k]) for s in succ[k]])
+    return prio
+
+
+def pack(seq, before, first):
+    busy = {e: [] for e in "vspgy"}
+    start = {}
+    for k in seq:
+        o = OPS[k]
+        t = max([start[j] + OPS[j]["cost"] + g for j, g in before[k]] + [first[k]])
+        line = busy[o["eng"]]
+        i = 0
+        while i < len(line) and line[i][0] < t + o["cost"]:
+            t = max(t, line[i][1])
+            i += 1
+        line.insert(i, (t, t + o["cost"]))
+        start[k] = t
+    return start
+
+
 def schedule():
     users = dependencies()
     n = len(OPS)
@@ -515,54 +683,37 @@ def schedule():
     for k, o in enumerate(OPS):
         for j in o["deps"]:
             succ[j].append(k)
-    prio = [0.0] * n
-    behind = {}
-    for k in range(n - 1, -1, -1):
-        o = OPS[k]
-        prio[k] = o["cost"] + o["lat"] + max([prio[s] + LAT for s in succ[k]] + [0.0])
-        key = (o["eng"], o["wr"][0][0]) if o["wr"] and o["wr"][0][0][:3] in ("cm_", "ce_", "xe_") else None
-        if key in behind:
-            prio[k] = max(prio[k], o["cost"] + behind[key])
-        if key:
-            behind[key] = prio[k]
-    for k in range(n):
-        prio[k] += 1000.0 * OFF.get(OPS[k]["tag"], 0)
+    prio = priorities(succ)
     left = [len(o["deps"]) for o in OPS]
     ready = [k for k in range(n) if left[k] == 0]
     free = {e: 0.0 for e in "vspgy"}
-    end = [0.0] * n
+    base = [0.0] * n
     holder = {b: None for b in range(8)}
     bound = {}
     todo = {nm: len(set(v)) for nm, v in users.items()}
     order = []
-
-    def avail(j, eng, hard):
-        if not hard:
-            return 0.0
-        return end[j] + OPS[j]["lat"] + (LATS if OPS[j]["eng"] == eng else LAT)
-
     while ready:
         cand = []
         for k in ready:
             o = OPS[k]
-            t = max([avail(j, o["eng"], h) for j, h in o["deps"].items()] + [0.0])
-            pick = None
-            ok = True
+            t, pick = base[k], None
             for nm in o["banks"]:
                 if nm not in bound:
-                    opts = [(0.0 if holder[b] is None else avail(users[holder[b]][-1], o["eng"], True), b)
-                            for b in POOLS[nm[1:4]] if holder[b] is None or todo[holder[b]] == 0]
-                    if opts:
-                        pick = (nm, min(opts)[1])
-                        t = max(t, min(opts)[0])
-                    else:
-                        ok = False
-            if ok:
+                    opts = []
+                    for b in POOLS[nm[1:4]]:
+                        if holder[b] is None:
+                            opts.append((0.0, b))
+                        elif todo[holder[b]] == 0:
+                            j = users[holder[b]][-1]
+                            opts.append((OPS[j]["t"] + OPS[j]["cost"] + gap(j, k, True), b))
+                    pick = (nm, min(opts)[1]) if opts else False
+                    t = max(t, min(opts)[0]) if opts else t
+            if pick is not False:
                 cand.append((max(t, free[o["eng"]]), k, pick))
         est = {c[1]: c[0] for c in cand}
         soon = {e: [] for e in free}
-        horizon = min(cand)[0] + 2000.0
-        seen = {}
+        horizon = min(cand)[0] + AHEAD
+        seen, late = {}, {}
         front = [c[1] for c in cand]
         while front:
             j = front.pop()
@@ -571,21 +722,17 @@ def schedule():
             soon[OPS[j]["eng"]].append(j)
             for k in succ[j]:
                 seen[k] = seen.get(k, 0) + 1
+                late[k] = max(late.get(k, base[k]), est[j] + OPS[j]["cost"] + gap(j, k, OPS[k]["deps"][j]))
                 if seen[k] == left[k]:
-                    o = OPS[k]
-                    t = free[o["eng"]]
-                    for i, h in o["deps"].items():
-                        t = max(t, est[i] + OPS[i]["cost"] + (OPS[i]["lat"] + LAT if h else 0) if i in est
-                                else avail(i, o["eng"], h))
-                    est[k] = t
+                    est[k] = late[k]
                     front.append(k)
         clear = [c for c in cand if not any(
-            prio[h] > prio[c[1]] + MARGIN and est[h] < c[0] + OPS[c[1]]["cost"] - SLACK for h in soon[OPS[c[1]]["eng"]])]
+            prio[h][0] > prio[c[1]][0] and OPS[h]["tag"] in URGENT and est[h] < c[0] + OPS[c[1]]["cost"] - SLACK
+            for h in soon[OPS[c[1]]["eng"]])]
         cand = clear or cand
         t0, k0, _ = min(cand)
         eng = OPS[k0]["eng"]
-        near = [c for c in cand if OPS[c[1]]["eng"] == eng and c[0] <= t0 + WIN]
-        t, k, pick = max(near, key=lambda c: prio[c[1]])
+        t, k, pick = max((c for c in cand if OPS[c[1]]["eng"] == eng and c[0] <= t0 + WIN), key=lambda c: prio[c[1]])
         o = OPS[k]
         if pick is not None:
             nm, b = pick
@@ -596,15 +743,25 @@ def schedule():
         for nm in o["banks"]:
             todo[nm] -= 1
         o["t"] = t
-        end[k] = t + o["cost"]
-        free[eng] = end[k]
+        free[eng] = t + o["cost"]
         order.append(k)
         ready.remove(k)
         for s in succ[k]:
+            base[s] = max(base[s], free[eng] + gap(k, s, OPS[s]["deps"][k]))
             left[s] -= 1
             if left[s] == 0:
                 ready.append(s)
-    return order, bound, max(end[k] + OPS[k]["lat"] for k in range(n))
+    pre = [[(j, gap(j, k, h)) for j, h in OPS[k]["deps"].items()] for k in range(n)]
+    post = [[] for _ in range(n)]
+    for k in range(n):
+        for j, g in pre[k]:
+            post[j].append((k, g))
+    back = pack(sorted(range(n), key=lambda k: (-(OPS[k]["t"] + OPS[k]["cost"]), -k)), post, [o["lat"] for o in OPS])
+    start = pack(sorted(range(n), key=lambda k: (-(back[k] + OPS[k]["cost"]), k)), pre, [0.0] * n)
+    for k, o in enumerate(OPS):
+        o["t"] = start[k]
+    order.sort(key=lambda k: start[k])
+    return order, bound, max(o["t"] + o["cost"] + o["lat"] for o in OPS)
 
 
 def waits(order):
@@ -641,7 +798,7 @@ def waits(order):
 program()
 ORDER, BANK, SPAN = schedule()
 waits(ORDER)
-SEMAPHORES = SEMS + ["h%d" % c for c in range(NCH)]
+SEMAPHORES = SEMS + ["h%d" % c for c in range(1, NCH)]
 
 
 def rank_program(g, core, T, topo):
@@ -665,11 +822,11 @@ def rank_program(g, core, T, topo):
                 dst = T.cores[(r - 2) % N]
                 rid, pid, _ = topo.addr(dst)
                 es = lanes(core, dst)
-                for c in range(NCH):
+                for c in range(1, NCH):
                     g.wait_ge(T.sem["h%d" % c], len(topo.engines(T.cores[r], core)[-8:]))
                     x = T.b_xw2[:, c * piece:(c + 1) * piece]
                     g.remote_dma(x, x, T.sem.xa, T.sem.sent, pid, rid, bits(es))
-                g.wait_ge(T.sem.sent, NCH * len(es))
+                g.wait_ge(T.sem.sent, (NCH - 1) * len(es))
         return
     queue = {"v": g.vector, "s": g.scalar, "p": g.tensor, "g": g, "y": g.sync}
 
@@ -703,18 +860,18 @@ def rank_program(g, core, T, topo):
                 q.wait_ge(T.sem["s" + d["eng"]], d["count"])
         args = [view(a) for a in o["args"]]
         if o["fn"] == "relay":
-            hp = helper(rank)
-            rid, pid, _ = topo.addr(hp)
-            es = topo.engines(core, hp)[-8:]
-            for c in range(NCH):
+            for c in (1, 0) + tuple(range(2, NCH)):
+                peer = helper(rank) if c else T.cores[(rank - 2) % N]
+                rid, pid, _ = topo.addr(peer)
+                es = topo.engines(core, peer)[-8:]
                 g.remote_dma(T.b_xw2[:, c * piece:(c + 1) * piece], T.b_xw[:, c * piece:(c + 1) * piece],
-                             T.sem["h%d" % c], T.sem.sent, pid, rid, bits(es))
+                             T.sem["h%d" % c] if c else T.sem.xa, T.sem.sent, pid, rid, bits(es))
                 sent += len(es)
         elif o["dst"] is not None:
             peer = T.cores[(rank + o["dst"]) % N]
             rid, pid, _ = topo.addr(peer)
             es = lanes(core, peer)
-            if len(args) == 3:
+            if len(args) > 2:
                 g.remote_dma_fused([RemoteDMATransfer(
                     dst_ids=[DstId(rid=rid, pnc=pid)], dma_engine_mask=bits(es), remote_sem=T.sem[o["sem"]],
                     srcs=args[1:], dsts=args[:1], alu_op=1)], local_sem=T.sem.sent)

from concourse.bass import DstId, RemoteDMATransfer
from concourse.mybir import AluOpType as ALU, ActivationFunctionType as ACT

V, S0, C, NT, N = 3072, 256, 96, 3, 8
AT, BT = (13, 12, 14), (11, 9, 10)
S = S0 + C * NT
HALF = 1536
BIG = 4096.0
H = 65536.0
FN = 3376
WS = 35
PAD = 16

NB = {"s0": 16, "s1": 10, "s2": 8, "d01": 16, "d02": 12, "d12": 8}
REP = {"s0": 2, "s1": 2, "s2": 2, "d01": 4, "d02": 2, "d12": 4}
SINGLE = {"s0": 0, "s1": 8, "s2": 4, "d01": 0, "d02": 0, "d12": 0}
ONS = "LV2 LV1 xls2 xed01 xed02 xed12 gn2 Wn1 Wn0 LV0 LV2d xld12 hb0".split()
FT = "F0 F0 F0".split()
FIRST = {"s0": 2, "s1": 0, "s2": 0, "d01": 0, "d02": 0, "d12": 0}
GR = 2
FGS = (2, 2, 1)
NCH = 4
FCH = 422
P = {"cy": 1.04, "cp": 0.55, "ga": 1.56, "sc": 3.8, "v0": 40.0, "s0": 80.0, "vi": 60.0, "lat": 110.0, "lats": 70.0,
     "hop": 2600.0, "issue": 700.0, "xlat": 16000.0, "dma": 2000.0, "bw": 190.0}
WIN = 30.0
SLACK = 450.0
AHEAD = 2000.0
RANK = "s0 md12 ms0 s2 dif ms1 es0 md01 p r0 s1 es1 r2 ed01 ms2 r1 f md02 rest ed02 es2 ed12 c f1".split()
RANK2 = "ms0 p s2 r0 ms1 es1 ms2 s1 md12 md01 s0 c f1 es0 r2 r1 ed12 md02 ed01 es2 f ed02".split()
URGENT = "s0 s1 ed12 ed02 c f ms2 md01 md12 es2 ms0".split()
POOLS = {"dif": [0, 1], "cnt": [2, 3, 4], "hld": [5], "log": [6, 7]}

JOBS = {
    "s0": (0, S0, "Qs", "Qs", 0, "xw"), "s1": (1, S0, "Qs1", "Qs1", 0, "xw"), "s2": (2, S0, "Qs", "Qs", 0, "xw2"),
    "d01": (1, C, "Qm01", "Qe01", S0, "xw"), "d02": (2, C, "Qm0", "Qe0", S0, "xw2"),
    "d12": (2, C, "Qm1", "Qe1", S0 + C, "xw2")}

BUF = {}


def _decl(names, cols, dtype):
    for nm in names.split():
        BUF[nm] = (cols, dtype)


_decl("xw xw2", V + 16, "bfloat16")
_decl("mi", 2 * S0, "int32")
_decl("M", PAD + S, "float32")
_decl("EA", PAD + S0 + C, "float32")
_decl("E LR YM YI", S, "float32")
_decl(" ".join(sorted(set(FT))), FN, "float32")
_decl("Qs Qs1", 2 * S0 + 16, "uint16")
_decl("Qm0 Qm1 Qm01", C + 6, "uint16")
_decl("Qe0 Qe1 Qe01", C, "uint16")
_decl("LV", S, "bfloat16")
_decl("TD0 TD1 TD2", S0 + 2 * C, "bfloat16")
for _j, _v in JOBS.items():
    _decl("xl_%s" % _j, REP[_j] * _v[1], "bfloat16")
    _decl("cm_%s ce_%s xe_%s" % (_j, _j, _j), 16 * _v[1], "bfloat16")
    if _v[0] == 1:
        _decl("am_%s ae_%s" % (_j, _j), _v[1], "bfloat16")
_decl("ZM ZE", 2 * S0 + 32, "float32")
_decl("ZD", 2 * C + 32, "float32")
_decl("GO", C + 2 * PAD, "float32")
_decl("W DG", S0, "float32")
_decl("R16 off rm", S0, "bfloat16")
_decl("N0 Mb", S0 + C, "bfloat16")
_decl("ASm ASe ABm ABe TM", S0 // 2, "bfloat16")
_decl("AM fine C96 old", C, "bfloat16")
_decl("RK", C, "float32")
_decl("hb", 48, "bfloat16")
_decl("cz", 48, "float32")
_decl("z al IDX", 6 * WS, "bfloat16")
_decl("TS IX", 6 * WS, "float32")
_decl("ids ll", 8 * NT, "uint16")
_decl("EG", C * NT, "uint16")
_decl("LG", C * NT, "float16")
_decl("gp gn df", C * NT, "bfloat16")
_decl("stay kept", C * NT, "float32")
_decl("FG", 16 * C * NT, "float16")
_decl("ali permd", 8, "uint16")
_decl("perm", 16, "uint16")
_decl("I NI IK BO SU MT", 128, "bfloat16")
_decl("BO32 NI32", 128, "float32")
_decl("R", 144, "float32")
_decl("B BN", 144, "bfloat16")
_decl("Bh", 144, "float16")
_decl("PI KI", 8, "int32")
_decl("PF CB low", 16, "float32")
_decl("Kc K1 K2 K3", 8, "float32")

SCRATCH = {"b_" + nm: ("sbuf", [128, c], d) for nm, (c, d) in BUF.items()}
for _b in range(8):
    SCRATCH["P%d" % _b] = ("psum", [128, 512], "float32")

OPS = []
TAG = [""]
SEMS = ["sv", "ss", "sp", "sg", "sent", "xa"]


def A(name, a=0, b=None, s=1):
    return ("ap", name, a, BUF[name][0] if b is None else b, s)


def IND(win, off):
    return ("ind", win, off)


def MM(a, b):
    return A("M", PAD + a, PAD + b)


def _isap(x):
    return isinstance(x, tuple) and x[0] in ("ap", "ind")


def _n(x):
    return 16 * _n(x[2]) if x[0] == "ind" else (x[3] - x[2] + x[4] - 1) // x[4]


def _ps(x):
    return _isap(x) and x[0] == "ap" and x[1][0] == "@"


def _two(x):
    return x[0] == "ap" and not _ps(x) and BUF[x[1]][1] in ("bfloat16", "float16", "uint16")


def _regs(x):
    return _regs(x[1]) + _regs(x[2]) if x[0] == "ind" else [(x[1], x[2], x[3])]


def op(eng, fn, outs, ins, args, cost, kw=None, lat=0.0, sem=None, dst=None):
    wr, rd = [], []
    for o in outs:
        if o[0] == "ind":
            wr += _regs(o[1])
            rd += _regs(o[2])
        else:
            wr += _regs(o)
    for i in ins:
        if _isap(i):
            rd += _regs(i)
    OPS.append({"eng": eng, "fn": fn, "args": args, "kw": kw or {}, "wr": wr, "rd": rd, "cost": cost, "lat": lat,
                "sem": sem, "dst": dst, "tag": TAG[0]})


def _vcost(out, in0, per):
    if out[0] == "ind":
        return P["vi"] + P["sc"] * _n(out) * P["cy"]
    if in0[0] == "ind":
        return P["vi"] + P["ga"] * _n(out) * P["cy"]
    return P["v0"] + max(64, per * _n(in0)) * P["cy"]


def tt(out, a, b, o):
    op("v", "tensor_tensor", [out], [a, b], [out, a, b, o], _vcost(out, a, 1 if _ps(a) or _ps(b) else 2))


def ts(out, a, s1, s2, o0, o1=None):
    args = [out, a, s1, s2, o0] + ([] if o1 is None else [o1])
    op("v", "tensor_scalar", [out], [a, s1, s2], args, _vcost(out, a, 0.5 if _two(out) and _two(a) else 1))


def cp(out, a):
    op("v", "tensor_copy", [out], [a], [out, a], _vcost(out, a, 0.5 if _two(out) and _two(a) else 1))


def ms(out, c):
    op("v", "memset", [out], [], [out, c], _vcost(out, out, 0.5 if _two(out) else 1))


def scan(out, d0, d1, init, o0, o1):
    two = _two(out) and _two(d0) and _two(d1)
    op("v", "tensor_tensor_scan", [out], [d0, d1], [out, d0, d1, init, o0, o1], _vcost(out, d0, 0.5 if two else 1))


def vtranspose(out, a):
    op("v", "transpose", [out], [a], [out, a], _vcost(out, a, 1))


def act(out, a, f, bias=0.0, scale=1.0):
    kw = {} if f == ACT.Copy else {"bias": bias, "scale": scale}
    cost = P["s0"] + (P["ga"] * _n(out) if a[0] == "ind" else max(64, _n(out))) * P["cy"]
    op("s", "activation", [out], [a, bias, scale], [out, a, f], cost, kw)


def relu(out, a, bias, name):
    if name in ONS:
        act(out, a, ACT.Relu, bias)
    else:
        ts(out, a, bias, 0.0, ALU.add, ALU.max)


def gather(out, a, name):
    if name in ONS:
        act(out, a, ACT.Copy)
    else:
        cp(out, a)


def after(name):
    OPS[-1]["after"] = [k for k, x in enumerate(OPS[:-1]) if x["wr"] and x["wr"][0][0] == name][-1]


def mm(out, l, r, start, stop):
    four = 4 if BUF[r[1]][1] == "float32" else 1
    op("p", "matmul", [out], [l, r], [out, l, r, start, stop], 10 + four * max(64, _n(r)) * P["cp"])


def iota(out, pat, base, cm):
    kw = {} if BUF[out[1]][1] == "int32" else {"allow_small_or_imprecise_dtypes": True}
    op("g", "iota", [out], [], [out, pat, base, cm], (156 + 2 * _n(out)) * P["cy"], kw)


def fill(out, c):
    iota(out, [[0, _n(out)]], int(c), 0)


def aff(out, a, pat, cmp_op, c, base, cm):
    op("g", "affine_select", [out], [a], [out, a, pat, cmp_op, c, base, cm], (205 + 2 * _n(out)) * P["cy"])


def dma(eng, out, a, nbytes, add=False):
    sem = "d%d" % len(SEMS)
    SEMS.append(sem)
    outs = [out] if out[1] in BUF else []
    ins = [a] if a[1] in BUF else []
    if add:
        op(eng, "dma_start", outs, ins + outs, [out, a], P["issue"], {"accum_op": ALU.add},
           P["dma"] + 200 + 2 * nbytes / P["bw"], sem)
    else:
        op(eng, "dma_start", outs, ins, [out, a], P["issue"] if eng == "g" else 80.0, lat=P["dma"] + nbytes / P["bw"], sem=sem)


def send(dst, out, *srcs):
    sem = "r%d" % len(SEMS)
    SEMS.append(sem)
    op("g", "remote_dma", [out], list(srcs), [out] + list(srcs), P["issue"],
       lat=P["hop"] + 256 * _n(out) / 60.0, sem=sem, dst=dst)


def col(name, c):
    return A(name, c, c + 1)


def sel(name, i):
    return A(name, 15 - i, 143 - i)


def per(name, t):
    w = BUF[name][0] // NT
    return A(name, w * t, w * t + (6 if w == 8 else w))


BIASCOL = {}


def constants():
    iota(col("PI", 0), [[0, 1]], 0, 1)
    iota(col("PI", 4), [[0, 1]], 0, 17)
    fill(A("BO32"), 1)
    aff(A("BO32"), A("BO32"), [[-16, 8], [0, 16]], ALU.is_ge, 0.0, 0, 1)
    aff(A("BO32"), A("BO32"), [[16, 8], [0, 16]], ALU.is_ge, 0.0, 15, -1)
    aff(A("MT"), A("BO32"), [[1, 128]], ALU.is_gt, 0.0, 0, -1)
    aff(A("SU"), A("BO32"), [[-1, 128]], ALU.is_gt, 0.0, 0, 1)
    iota(A("R"), [[1, 144]], 0, 0)
    ts(col("PI", 1), col("PI", 0), 15, None, ALU.bitwise_and)
    ts(col("PI", 2), col("PI", 0), 112, None, ALU.bitwise_and)
    ts(col("PI", 3), col("PI", 4), 4, 1, ALU.logical_shift_right, ALU.bitwise_and)
    cp(A("PF", 0, 4), A("PI", 0, 4))
    pb, pg, odd = col("PF", 1), col("PF", 2), col("PF", 3)
    ts(A("I"), A("R", 0, 128), col("PF", 0), None, ALU.is_equal)
    ts(A("B"), A("R"), pg, 15.0, ALU.subtract, ALU.is_equal)
    act(A("NI32"), A("I"), ACT.Identity, 0.0, -1.0)
    act(A("NI"), A("I"), ACT.Identity, 0.0, -1.0)
    act(A("IK"), A("I"), ACT.Identity, 0.0, BIG)
    act(A("BN"), A("B"), ACT.Identity, 0.0, -BIG)
    act(A("Bh"), A("B"), ACT.Identity, 0.0, 1.0 / 16)
    act(A("BO"), A("BO32"), ACT.Copy)
    act(col("PF", 4), odd, ACT.Identity, 0.0, float(S0 + 16))
    act(col("PF", 5), pb, ACT.Identity, col("PF", 4), 16.0)
    ts(A("perm"), A("R", 0, 16), col("PF", 5), None, ALU.add)
    act(A("Kc", 0, 6), A("R", 0, C, 16), ACT.Identity, pb)
    ts(A("K1", 0, 6), A("Kc", 0, 6), -2.5, 1.0 / 6, ALU.add, ALU.mult)
    cp(A("KI", 0, 6), A("K1", 0, 6))
    act(col("PF", 6), odd, ACT.Identity, 0.0, float(C + 16))
    act(A("K2", 0, 6), A("Kc", 0, 6), ACT.Identity, col("PF", 6), 16.0)
    ts(A("K1", 0, 6), A("KI", 0, 6), -95.0, None, ALU.mult)
    tt(A("K3", 0, 6), A("K1", 0, 6), A("K2", 0, 6), ALU.add)
    cp(A("permd", 0, 6), A("K3", 0, 6))
    iota(A("R16"), [[0, 16], [1, 16]], 0, 0)
    ts(A("off"), A("R16"), pb, -2 * BIG, ALU.not_equal, ALU.mult)
    act(A("rm"), A("R16"), ACT.Sign)
    fill(A("TS"), -30000)
    act(A("TS", 0, 6 * WS, WS), A("Kc", 0, 6), ACT.Identity, 0.5)
    iota(A("IX"), [[0, 6], [1, WS]], 0, 0)
    act(A("IDX"), A("IX"), ACT.Identity, 0.0, 1.0 / 256)
    act(A("RK"), A("R", 0, C), ACT.Identity, col("TS", 0), -1.0)
    fill(A("hb", 1, WS), -1)
    fill(col("hb", 0), 0)
    fill(A("C96"), HALF // 16)
    ms(col("CB", 0), 2.0 ** -112)
    act(col("CB", 1), pb, ACT.Identity, float(V), -H)
    for j, v in JOBS.items():
        key = (NB.get(j, 16), AT[v[0]], j == "s1")
        if key not in BIASCOL:
            a = key[1]
            one = 1.0 if key[2] else 0.0
            if key[0] == 16:
                BIASCOL[key] = 2 * BIG * (a - 8) - one
                continue
            c = col("CB", 2 + len(BIASCOL))
            BIASCOL[key] = c
            ts(c, pb, float(key[0]), BIG * (a - 16), ALU.is_lt, ALU.mult)
            act(c, c, ACT.Identity, BIG * a - one)
    ms(A("low"), -2.0 ** 99)
    act(A("xw", V), A("low"), ACT.Identity, 0.0, 4.0)
    act(A("xw2", V), A("low"), ACT.Identity, 0.0, 4.0)
    ms(A("M", 0, PAD), 0.0)
    ms(MM(S0, S0 + PAD), H)
    fill(MM(S0 + PAD, S), H)
    ms(A("EA", 0, PAD), 0.0)
    ms(A("EA", PAD + S0), float(V))
    fill(A("E", S0), V)
    fill(A("YI", S - C), V)
    fill(A("LV", S0), 0)
    fill(A("N0", S0), 0)
    fill(A("TD0", S0, S0 + C), BIG)
    fill(A("TD1", S0 + C), 0)
    fill(A("GO", 0, PAD), 0)
    fill(A("GO", PAD + C), 0)
    iota(A("LR", S0), [[1, S - S0]], V + 1 - HALF, 0)


def names():
    for f in sorted(set(FT)):
        TAG[0] = "f" if f == FT[0] else "f1"
        w = FCH if f == FT[0] else FCH // 2
        for a in range(0, FN, w):
            iota(A(f, a, a + w), [[1, w]], a - HALF, 0)


def leaders(src, none, n, tag, lr, lst):
    pa, pb = A("@log" + tag + "a", 0, n), A("@log" + tag + "b", 0, n)
    mm(pa, A("MT"), none, True, False)
    mm(pa, A("NI32"), src, False, True)
    relu(A("W", 0, n), pa, col("CB", 1), "W" + tag)
    if lst is not None:
        mm(pb, A("BO32"), A("W", 0, n), True, False)
        mm(pb, A("I"), A("off", 0, n), False, True)
        scan(A("DG", 0, n), A("rm", 0, n), pb, 0.0, ALU.mult, ALU.max)
        ts(lst, A("DG", 15, n, 16), -1.0, float(V), ALU.mult, ALU.add)
    mm(pa, A("BO32"), A("W", 0, n), True, True)
    act(lr, pa, ACT.Identity, float(V - HALF), -1.0)


def turn(out, src, z, n, perm):
    vtranspose(A(z, 0, n), A(src, PAD, PAD + n))
    vtranspose(A(z, n, 2 * n + 32), A(src, 0, n + 32))
    ts(out, IND(A(z), perm), float(V), None, ALU.min)


def prepare():
    dma("y", A("mi", 0, S0), ("ap", "mem0", 0, S0, 1), 131072)
    dma("s", A("mi", S0), ("ap", "inv0", 0, S0, 1), 131072)
    dma("y", A("xw", 0, V), ("ap", "xs", 0, V, 1), 786432 + 262144)
    OPS[-1]["after"] = len(OPS) - 3
    ts(A("N0", 0, S0), A("mi", 0, S0), float(V), H, ALU.is_ge, ALU.mult)
    cp(MM(0, S0), A("mi", 0, S0))
    leaders(MM(0, S0), A("N0", 0, S0), S0, "p", A("LR", 0, S0), A("Qs", 2 * S0))
    turn(A("Qs", 0, S0), "M", "ZM", S0, A("perm"))
    cp(A("EA", PAD, PAD + S0), A("mi", S0))
    turn(A("Qs", S0, 2 * S0), "EA", "ZE", S0, A("perm"))
    dma("y", A("E", 0, S0), A("EA", PAD, PAD + S0), 131072)
    send(1, A("Qs1"), A("Qs"))
    op("g", "relay", [A("xw2", 0, V)], [A("xw", 0, V)], [], NCH * P["issue"], lat=P["xlat"], sem="xa", dst=-2)


def compare(j, out, q, o, rows, alu):
    _, n, _, _, _, xw = JOBS[j]
    k = n // 16
    i = rows[0]
    while i < rows[1]:
        r = 1 if i >= 16 - SINGLE[j] or i < FIRST[j] else min(REP[j], rows[1] - i)
        tt(A(out, i * n, (i + r) * n), IND(A(xw), A(q, o + i * k, o + (i + r) * k)), A("xl_" + j, 0, r * n), alu)
        i += r


def answer(out, a):
    send(-1, A(out), A(a, 0, S0 // 2), A(a, 0, S0 // 2), A(a, S0 // 2, S0))


def second(out, src, tmp):
    act(A(tmp), A(src), ACT.Abs, 1.0)
    act(out, A(tmp), ACT.Abs, -BIG, BIG / 2)


def members(j):
    t, n, q, _, s0, xw = JOBS[j]
    o = 2 * S0 if n == S0 else C
    xl = "xl_" + j
    gather(A(xl, 0, n), IND(A(xw), A(q, o, o + n // 16)), "xl" + j)
    for r in range(1, REP[j]):
        if j in ("s0", "d01", "d12"):
            gather(A(xl, r * n, (r + 1) * n), A(xl, 0, n), "xl" + j)
        else:
            dma("y", A(xl, r * n, (r + 1) * n), A(xl, 0, n), 256 * n)
    compare(j, "cm_" + j, q, 0, (0, 16), ALU.is_equal)
    held = j in ("s2", "d02")
    cnt = A("@hld", s0, s0 + n) if held else A(("@log" if n == C else "@hld") + j, 0, n)
    opened = held or j == "s0"
    if j == "s0":
        mm(cnt, A("NI"), A("N0", 0, n), True, False)
    if j == "s2":
        mm(A("@hld", 0, S0 + C), A("NI"), A("N0"), True, False)
        after("@hldl")
    for i in range(16):
        mm(cnt, sel("BN", i), A("cm_" + j, i * n, (i + 1) * n), i == 0 and not opened, i == 15 and t < 2)
    if j == "s0":
        relu(A("LV", 0, n), cnt, BIG * BT[t], "LV0")
    elif j == "s1":
        act(A("am_s1"), cnt, ACT.Sign, BIG * BT[t] - 1.0)
        answer("ASm", "am_s1")
    elif j == "d01":
        relu(A("am_d01"), cnt, BIG * BT[t], "am")
        send(-1, A("AM"), A("am_d01"))


def bounds(j):
    t, n, _, q, s0, xw = JOBS[j]
    xl, xe, ce = "xl_" + j, "xe_" + j, "ce_" + j
    cnt = A("@cnte" + j, 0, n)
    nb = NB.get(j, 16)
    if n == S0:
        for i in range(0, nb, GR):
            e = min(nb, i + GR)
            act(A(xe, i * n, e * n), IND(A(xw), A(q, S0 + 16 * i, S0 + 16 * e)), ACT.Copy)
        for i in range(0, nb, 2):
            w = min(2, nb - i) * n
            bank = A("@dif%s_%d" % (j, i), 0, w)
            mm(bank, A("I"), A(xe, i * n, i * n + w), True, False)
            mm(bank, A("NI"), A(xl, 0, w), False, True)
            act(A(ce, i * n, i * n + w), bank, ACT.Sign, col("CB", 0))
        compare(j, ce, q, S0, (nb, 16), ALU.is_ge)
    else:
        act(A(xe, 0, 8 * C), IND(A(xw), A(q, 0, C // 2)), ACT.Copy)
        gather(A(xe, 8 * C), IND(A(xw), A(q, C // 2)), "xe" + j)
        for i in range(0, nb, 4):
            bank = "@dif%s_%d" % (j, i)
            for z in range(4):
                mm(A(bank, z * n, (z + 1) * n), A("I"), A(xe, i + z, 16 * n, 16), True, False)
                mm(A(bank, z * n, (z + 1) * n), A("NI"), A(xl, 0, n), False, True)
            act(A(ce, i * n, (i + 4) * n), A(bank, 0, 4 * n), ACT.Sign, col("CB", 0))
        if nb < 16:
            mm(A("@difx" + j, 0, n), A("I"), A(xl, 0, n), True, True)
        for i in range(nb, 16):
            tt(A(ce, i * n, (i + 1) * n), A(xe, i, 16 * n, 16), A("@difx" + j, 0, n), ALU.is_ge)
    for i in range(16):
        mm(cnt, sel("BN", i), A(ce, i * n, (i + 1) * n), i == 0, i == 15)
    bias = BIASCOL[(nb, AT[t], j == "s1")]
    home = A("TD%d" % t, s0, s0 + n)
    if j == "s1":
        act(A("ae_s1"), cnt, ACT.Sign, bias)
        answer("ASe", "ae_s1")
    elif j == "d01":
        act(A("ae_d01"), cnt, ACT.Relu, bias)
        send(-1, home, A("ae_d01"))
    else:
        act(home, cnt, ACT.Relu, bias)


def positions(t):
    n = S0 + C * t
    na = n // 16
    h, u, f = A("@logh%d" % t, 0, na), "@logu%d" % t, A("@logi%d" % t, 0, 6)
    for b in range(16):
        mm(h, sel("BN", b), A("LV", b, n, 16), b == 0, b == 15)
    if "hb%d" % t in ONS:
        act(A("hb", 1, 1 + na), h, ACT.Sign)
    else:
        ts(A("hb", 1, 1 + na), h, -1.0, None, ALU.max)
    for c in range(6):
        mm(A(u, WS * c, WS * (c + 1)), A("BO"), A("hb", 0, WS), True, True)
    mm(A(u, 256, 256 + WS - 1), A("SU"), A("hb", 1, WS), True, True)
    scan(A("z"), A(u, 0, 6 * WS), A("TS"), 0.0, ALU.add, ALU.max)
    scan(A("al"), A("z"), A("IDX"), 0.0, ALU.max, ALU.min)
    last = A("al", WS - 1, 6 * WS, WS)
    ts(A("ali", 0, 6), last, 256.0, None, ALU.mult)
    tt(A("cz", 0, WS - 1), A("z", 1, WS), A(u, 256, 256 + WS - 1), ALU.subtract)
    tt(A("fine"), IND(A("cz", 0, WS - 1), A("ali", 0, 6)), A("RK"), ALU.is_ge)
    for b in range(16):
        mm(f, sel("B", b), A("fine", b, C, 16), b == 0, False)
    mm(f, A("IK"), last, False, True)
    cp(per("ids", t), f)


def leavers(t):
    if t == 1:
        h = S0 // 2
        second(A("TM"), "ASm", "ABm")
        dma("g", A("Mb", 0, S0), MM(0, S0), 65536)
        mm(A("@hldl", 0, S0), A("NI"), A("Mb", 0, S0), True, False)
        after("am_s1")
        mm(A("@hldl", 0, S0), A("NI"), A("N0", 0, S0), False, False)
        mm(A("@hldl", 0, h), A("IK"), A("ASm"), False, False)
        mm(A("@hldl", h, S0), A("I"), A("TM"), False, True)
        relu(A("LV", 0, S0), A("@hldl", 0, S0), 0.0, "LV1")
        tt(A("LV", S0, S0 + C), A("AM"), per("gn", 0), ALU.is_gt)
    if t == 2:
        dma("g", A("Mb"), MM(0, S0 + C), 90112)
        mm(A("@hld", 0, S0 + C), A("NI"), A("Mb"), False, True)
        relu(A("LV", 0, S0 + C), A("@hld", 0, S0 + C), BIG * BT[t], "LV2")
        mm(A("@logd12", 0, C), A("NI"), per("gn", 1), False, True)
        relu(A("LV", S0 + C, S0 + 2 * C), A("@logd12", 0, C), BIG * BT[t], "LV2d")


def split(t):
    n = S0 + C * t
    last = t == NT - 1
    ids, go, gn = per("ids", t), A("GO", PAD, PAD + C), per("gn", t)
    leavers(t)
    positions(t)
    if "gn%d" % t in ONS:
        act(gn, IND(A("LV", 0, n + C), ids), ACT.Relu, H, -H)
    else:
        ts(gn, IND(A("LV", 0, n + C), ids), 0.0, H, ALU.is_le, ALU.mult)
    tt(go, IND(MM(0, n + C), ids), gn, ALU.add)
    act(per("LG", t), IND(A("LR", 0, n + C), ids), ACT.Copy)
    leaders(go, gn, C, "n%d" % t, A("LR", n, n + C), None if last else A("Qm%d" % t, C))
    if not last:
        turn(A("Qm%d" % t, 0, C), "GO", "ZD", C, A("permd", 0, 6))
    if t == 0:
        send(1, A("Qm01"), A("Qm0"))
    act(per("gp", t), gn, ACT.Identity, H, -1.0)
    tt(per("stay", t), IND(MM(0, n + C), ids), per("gp", t), ALU.add)
    cp(IND(MM(0, n + C), ids), per("stay", t))
    if last:
        ts(A("YM", 0, n), MM(0, n), float(V), None, ALU.min)
        ts(A("YM", n, S), go, float(V), None, ALU.min)
        dma("y", ("ap", "ym", 0, S, 1), A("YM"), 278528)
    else:
        dma("y", MM(n, n + C), go, 49152)
    bank = A("@logl%d" % t, 0, 6)
    for b in range(16):
        mm(bank, sel("Bh", b), A("LG", C * t + b, C * (t + 1), 16), b == 0, b == 15)
    ts(per("ll", t), bank, float(HALF), None, ALU.add)


def deaths(t):
    if t == 1:
        act(A("TD1", 0, S0 // 2), A("ASe"), ACT.Relu, 0.0, BIG)
        second(A("TD1", S0 // 2, S0), "ASe", "ABe")
    if t == 2:
        for a, b in ((0, S0), (S0, S0 + C), (S0 + C, S0 + 2 * C)):
            bank = A("@cnty%d" % a, 0, b - a)
            mm(bank, A("NI"), A("TD2", a, b), True, False)
            mm(bank, A("NI32"), A("E", a, b), False, True)
            ts(A("YI", a, b), bank, -1.0, float(V), ALU.mult, ALU.min)


def rename(t):
    n = S0 + C * t
    last = t == NT - 1
    ids, ll, f, df, kept = per("ids", t), per("ll", t), FT[t], per("df", t), per("kept", t)
    cp(IND(A(f), ll), A("LR", n, n + C))
    ts(per("EG", t), IND(A("EA", PAD) if t == 0 else A("E", 0, n + C), ids), float(V), None, ALU.min)
    if t == 1:
        ts(A("old"), IND(A("E", 0, n + C), ids), float(V), float(V), ALU.is_ge, ALU.mult)
    deaths(t)
    h = C // 2
    for z, a in enumerate((C * t, C * t + h)):
        if z < FGS[t]:
            act(A("FG", 16 * a, 16 * (a + h)), IND(A(f), A("EG", a, a + h)), ACT.Copy)
        else:
            cp(A("FG", 16 * a, 16 * (a + h)), IND(A(f), A("EG", a, a + h)))
    if f in FT[t + 1:]:
        cp(IND(A(f), ll), per("LG", t))
    if t == 1:
        tt(df, IND(A("TD1"), ids), A("old"), ALU.max)
    else:
        ts(df, IND(A("YI") if last else A("TD0", 0, n + C), ids), float(V), float(V), ALU.is_ge, ALU.mult)
    if not last:
        dma("g", A("E", 0, n), A("TD%d" % t, 0, n), 512 * n, True)
    tt(kept, df, per("stay", t), ALU.min)
    bank = A("@logf%d" % t, 0, C)
    for i in range(16):
        mm(bank, sel("Bh", i), A("FG", 16 * C * t + i, 16 * C * (t + 1), 16), i == 0, False)
    mm(bank, A("BO"), A("C96"), False, False)
    mm(bank, A("NI"), df, False, True)
    if last:
        dma("y", ("ap", "yi", 0, n, 1), A("YI", 0, n), 229376)
        tt(A("YI", n, S), bank, kept, ALU.max)
        dma("s", ("ap", "yi", n, S, 1), A("YI", n, S), 49152)
    else:
        tt(A("E", n, n + C), bank, kept, ALU.max)
        ts(A("Qe%d" % t), A("E", n, n + C), float(V), None, ALU.min)
        if t == 0:
            send(1, A("Qe01"), A("Qe0"))


def program():
    steps = [("c", constants, None), ("p", prepare, None), ("f", names, None)]
    for j in ("s0", "s1", 0, "d01", 1, "s2", "d02", "d12", 2):
        steps += [("m", members, j), ("e", bounds, j)] if j in JOBS else [("s", split, j), ("r", rename, j)]
    for tag, f, x in steps:
        TAG[0] = tag + ("" if x is None else str(x))
        if x is None:
            f()
        else:
            f(x)


def dependencies():
    hist = {}
    for k, o in enumerate(OPS):
        deps = {}
        acc = [(r, True) for r in o["wr"]] + [(r, False) for r in o["rd"]]
        for (nm, a, b), w in acc:
            for (j, a2, b2, w2) in hist.get(nm, []):
                same = OPS[j]["eng"] == o["eng"] and OPS[j]["sem"] is None
                if nm[0] == "@" or (a < b2 and a2 < b and (w or w2)):
                    deps[j] = deps.get(j, False) or not same or ((w or w2) and o["eng"] != "p")
        for (nm, a, b), w in acc:
            hist.setdefault(nm, []).append((k, a, b, w))
        if "after" in o:
            deps.setdefault(o["after"], False)
        o["deps"] = deps
        o["banks"] = sorted(set(r[0] for r, w in acc if r[0][0] == "@"))
    return {nm: [h[0] for h in v] for nm, v in hist.items() if nm[0] == "@"}


def gap(j, k, hard):
    if not hard:
        return 0.0
    return OPS[j]["lat"] + (P["lats"] if OPS[j]["eng"] == OPS[k]["eng"] else P["lat"])


def priorities(succ):
    n = len(OPS)
    way = [0.0] * n
    for k in range(n - 1, -1, -1):
        o = OPS[k]
        way[k] = o["cost"] + max([way[s] + gap(k, s, OPS[s]["deps"][k]) for s in succ[k]] + [o["lat"]])
    prio = []
    for k, o in enumerate(OPS):
        name = o["wr"][0][0] if o["wr"] else ""
        rank = RANK.index(o["tag"])
        if name[:3] in ("xe_", "cm_") or name == "FG" or o["tag"][0] == "f" or (
                name[:3] == "ce_" and o["rd"][0][0][0] != "@"):
            prio.append((-rank, 0, -k))
        else:
            dif = name[:4] == "@dif"
            prio.append((-min(rank, RANK.index("dif" if dif else "rest")), 1, -RANK2.index(o["tag"]),
                         -k if dif else way[k]))
    for k in range(n - 1, -1, -1):
        if OPS[k]["tag"] == "c":
            prio[k] = max([prio[k]] + [(prio[s][0], 3, 0, way[k]) for s in succ[k]])
    return prio


def pack(seq, before, first):
    busy = {e: [] for e in "vspgy"}
    start = {}
    for k in seq:
        o = OPS[k]
        t = max([start[j] + OPS[j]["cost"] + g for j, g in before[k]] + [first[k]])
        line = busy[o["eng"]]
        i = 0
        while i < len(line) and line[i][0] < t + o["cost"]:
            t = max(t, line[i][1])
            i += 1
        line.insert(i, (t, t + o["cost"]))
        start[k] = t
    return start


def schedule():
    users = dependencies()
    n = len(OPS)
    succ = [[] for _ in range(n)]
    for k, o in enumerate(OPS):
        for j in o["deps"]:
            succ[j].append(k)
    prio = priorities(succ)
    left = [len(o["deps"]) for o in OPS]
    ready = [k for k in range(n) if left[k] == 0]
    free = {e: 0.0 for e in "vspgy"}
    base = [0.0] * n
    holder = {b: None for b in range(8)}
    bound = {}
    todo = {nm: len(set(v)) for nm, v in users.items()}
    order = []
    while ready:
        cand = []
        for k in ready:
            o = OPS[k]
            t, pick = base[k], None
            for nm in o["banks"]:
                if nm not in bound:
                    opts = []
                    for b in POOLS[nm[1:4]]:
                        if holder[b] is None:
                            opts.append((0.0, b))
                        elif todo[holder[b]] == 0:
                            j = users[holder[b]][-1]
                            opts.append((OPS[j]["t"] + OPS[j]["cost"] + gap(j, k, True), b))
                    pick = (nm, min(opts)[1]) if opts else False
                    t = max(t, min(opts)[0]) if opts else t
            if pick is not False:
                cand.append((max(t, free[o["eng"]]), k, pick))
        est = {c[1]: c[0] for c in cand}
        soon = {e: [] for e in free}
        horizon = min(cand)[0] + AHEAD
        seen, late = {}, {}
        front = [c[1] for c in cand]
        while front:
            j = front.pop()
            if est[j] > horizon:
                continue
            soon[OPS[j]["eng"]].append(j)
            for k in succ[j]:
                seen[k] = seen.get(k, 0) + 1
                late[k] = max(late.get(k, base[k]), est[j] + OPS[j]["cost"] + gap(j, k, OPS[k]["deps"][j]))
                if seen[k] == left[k]:
                    est[k] = late[k]
                    front.append(k)
        clear = [c for c in cand if not any(
            prio[h][0] > prio[c[1]][0] and OPS[h]["tag"] in URGENT and est[h] < c[0] + OPS[c[1]]["cost"] - SLACK
            for h in soon[OPS[c[1]]["eng"]])]
        cand = clear or cand
        t0, k0, _ = min(cand)
        eng = OPS[k0]["eng"]
        t, k, pick = max((c for c in cand if OPS[c[1]]["eng"] == eng and c[0] <= t0 + WIN), key=lambda c: prio[c[1]])
        o = OPS[k]
        if pick is not None:
            nm, b = pick
            if holder[b] is not None:
                o["deps"][users[holder[b]][-1]] = True
            holder[b] = nm
            bound[nm] = b
        for nm in o["banks"]:
            todo[nm] -= 1
        o["t"] = t
        free[eng] = t + o["cost"]
        order.append(k)
        ready.remove(k)
        for s in succ[k]:
            base[s] = max(base[s], free[eng] + gap(k, s, OPS[s]["deps"][k]))
            left[s] -= 1
            if left[s] == 0:
                ready.append(s)
    pre = [[(j, gap(j, k, h)) for j, h in OPS[k]["deps"].items()] for k in range(n)]
    post = [[] for _ in range(n)]
    for k in range(n):
        for j, g in pre[k]:
            post[j].append((k, g))
    back = pack(sorted(range(n), key=lambda k: (-(OPS[k]["t"] + OPS[k]["cost"]), -k)), post, [o["lat"] for o in OPS])
    start = pack(sorted(range(n), key=lambda k: (-(back[k] + OPS[k]["cost"]), k)), pre, [0.0] * n)
    for k, o in enumerate(OPS):
        o["t"] = start[k]
    order.sort(key=lambda k: start[k])
    return order, bound, max(o["t"] + o["cost"] + o["lat"] for o in OPS)


def waits(order):
    know = {e: {} for e in "vspgy"}
    pos = {e: 0 for e in "vspgy"}
    for k in order:
        o = OPS[k]
        kn = know[o["eng"]]
        need = []
        for j in sorted((j for j, h in o["deps"].items() if h), key=lambda j: -OPS[j]["t"]):
            d = OPS[j]
            key = d["sem"] or d["eng"]
            if kn.get(key, -1) >= d["pos"]:
                continue
            need.append(j)
            kn[key] = d["pos"]
            d["mark"] = True
            if d["dst"] is None:
                for a, b in d["clock"].items():
                    if kn.get(a, -1) < b:
                        kn[a] = b
        o["need"] = need
        o["pos"] = pos[o["eng"]]
        pos[o["eng"]] += 1
        o["clock"] = dict(kn)
    count = {e: 0 for e in "vspg"}
    for k in order:
        o = OPS[k]
        if o["sem"] is None and o.get("mark"):
            count[o["eng"]] += 1
            o["count"] = count[o["eng"]]


program()
ORDER, BANK, SPAN = schedule()
waits(ORDER)
SEMAPHORES = SEMS + ["h%d" % c for c in range(1, NCH)]


def rank_program(g, core, T, topo):
    rank = T.rank_of(core)

    def lanes(src, dst):
        return topo.engines(src, dst)[:8]

    def bits(es):
        return sum(1 << e for e in es)

    def helper(r):
        src, dst = T.cores[r], T.cores[(r - 2) % N]
        return [c for c in topo.cores_of(src) if T.rank_of(c) is None and topo.die(c) == topo.die(src)
                and topo.may_write(c, dst)][0]

    piece = V // NCH
    if rank is None:
        for r in range(N):
            if helper(r) == core:
                dst = T.cores[(r - 2) % N]
                rid, pid, _ = topo.addr(dst)
                es = lanes(core, dst)
                for c in range(1, NCH):
                    g.wait_ge(T.sem["h%d" % c], len(topo.engines(T.cores[r], core)[-8:]))
                    x = T.b_xw2[:, c * piece:(c + 1) * piece]
                    g.remote_dma(x, x, T.sem.xa, T.sem.sent, pid, rid, bits(es))
                g.wait_ge(T.sem.sent, (NCH - 1) * len(es))
        return
    queue = {"v": g.vector, "s": g.scalar, "p": g.tensor, "g": g, "y": g.sync}

    def view(x):
        if not _isap(x):
            return x
        if x[0] == "ind":
            return view(x[1]).indirect(view(x[2]))
        buf = T["P%d" % BANK[x[1]]] if x[1][0] == "@" else T[("b_" if x[1] in BUF else "") + x[1]]
        return buf[:, x[2]:x[3]:x[4]] if x[4] != 1 else buf[:, x[2]:x[3]]

    calls = {
        "tensor_tensor": g.vector.tensor_tensor, "tensor_scalar": g.vector.tensor_scalar,
        "tensor_copy": g.vector.tensor_copy, "memset": g.vector.memset,
        "tensor_tensor_scan": g.vector.tensor_tensor_scan, "transpose": g.vector.transpose,
        "activation": g.scalar.activation, "matmul": g.tensor.matmul,
        "iota": g.iota, "affine_select": g.affine_select}
    sent = 0
    for k in ORDER:
        o = OPS[k]
        q = queue[o["eng"]]
        for j in o["need"]:
            d = OPS[j]
            if d["fn"] == "relay":
                q.wait_ge(T.sem.xa, NCH * len(lanes(helper((rank + 2) % N), core)))
            elif d["dst"] is not None:
                q.wait_ge(T.sem[d["sem"]], len(lanes(T.cores[(rank - d["dst"]) % N], core)))
            elif d["sem"] is not None:
                q.wait_ge(T.sem[d["sem"]], 16)
            else:
                q.wait_ge(T.sem["s" + d["eng"]], d["count"])
        args = [view(a) for a in o["args"]]
        if o["fn"] == "relay":
            for c in (1, 0) + tuple(range(2, NCH)):
                peer = helper(rank) if c else T.cores[(rank - 2) % N]
                rid, pid, _ = topo.addr(peer)
                es = topo.engines(core, peer)[-8:]
                g.remote_dma(T.b_xw2[:, c * piece:(c + 1) * piece], T.b_xw[:, c * piece:(c + 1) * piece],
                             T.sem["h%d" % c] if c else T.sem.xa, T.sem.sent, pid, rid, bits(es))
                sent += len(es)
        elif o["dst"] is not None:
            peer = T.cores[(rank + o["dst"]) % N]
            rid, pid, _ = topo.addr(peer)
            es = lanes(core, peer)
            if len(args) > 2:
                g.remote_dma_fused([RemoteDMATransfer(
                    dst_ids=[DstId(rid=rid, pnc=pid)], dma_engine_mask=bits(es), remote_sem=T.sem[o["sem"]],
                    srcs=args[1:], dsts=args[:1], alu_op=1)], local_sem=T.sem.sent)
            else:
                g.remote_dma(args[0], args[1], T.sem[o["sem"]], T.sem.sent, pid, rid, bits(es))
            sent += len(es)
        elif o["sem"] is not None:
            q.dma_start(args[0], args[1], **o["kw"]).then_inc(T.sem[o["sem"]], 16)
        else:
            ins = calls[o["fn"]](*args, **{a: view(b) for a, b in o["kw"].items()})
            if o.get("mark"):
                ins.then_inc(T.sem["s" + o["eng"]], 1)
    g.wait_ge(T.sem.sent, sent)
    for o in OPS:
        if o["sem"] is not None and o["dst"] is None and not o.get("mark"):
            g.sync.wait_ge(T.sem[o["sem"]], 16)
